import numpy as np
import ml_dtypes


def mxq(x, axis, fmt="e4m3"):
    dtype, down = {"e4m3": (ml_dtypes.float8_e4m3fn, 7), "e5m2": (ml_dtypes.float8_e5m2, 14)}[fmt]
    v = np.moveaxis(np.asarray(x, np.float32).astype(ml_dtypes.bfloat16).astype(np.float64), axis, -1)
    blocks = v.reshape(v.shape[:-1] + (-1, 32))
    amax = np.abs(blocks).max(-1, keepdims=True)
    byte = np.maximum(np.where(amax > 0, np.frexp(amax)[1] - 1 + 127, 0) - down, 1)
    scale = np.exp2(byte - 127.0)
    codes = (blocks / scale).astype(np.float32).astype(dtype).astype(np.float64)
    return np.moveaxis((codes * scale).reshape(v.shape), -1, axis)


WIDE = False


def mx_kscale(k):
    if not WIDE:
        return np.ones(k)
    levels = np.array([24, -24, 12, -12, 0])
    if k % 512:
        return np.exp2(np.random.permutation(np.resize(levels, k // 32))).repeat(32)
    a = np.empty((k // 512, 16))
    for p in range(k // 512):
        a[p, :8] = np.random.permutation(np.resize(levels, 8))
        for g in range(8):
            far = levels[np.abs(levels - a[p, g]) >= 10]
            a[p, g + 8] = far[np.random.randint(len(far))]
    return np.exp2(a.ravel()).repeat(32)


def f64(x):
    return np.asarray(x).astype(np.float64)


def striped(idx):
    return np.tile(idx.reshape(-1, 16).T, (8, 1)).astype(np.uint16)


def unstriped(offs):
    return offs[:16].T.reshape(-1).astype(np.int64)


E2M1 = np.array([0.0, 0.5, 1.0, 1.5, 2.0, 3.0, 4.0, 6.0, -0.0, -0.5, -1.0, -1.5, -2.0, -3.0, -4.0, -6.0])


def pack_weight(w, fmt):
    k, n = w.shape
    w = f64(np.asarray(w, np.float32).astype(ml_dtypes.bfloat16)).reshape(k // 32, 32, n)
    amax = np.abs(w).max(1)
    if fmt == "e4m3":
        byte = np.frexp(amax)[1] - 1 + 127 - 7
    else:
        mant, ex = np.frexp(amax / 6.0)
        byte = np.where(mant > 0.5, ex, ex - 1) + 127
    byte = np.clip(np.where(amax > 0, byte, 1), 1, 254)
    scaled = (w * np.exp2(127.0 - byte)[:, None, :]).reshape(k, n).astype(np.float32)
    by_word = np.ascontiguousarray(scaled.reshape(k // 512, 128, 4, n).transpose(0, 1, 3, 2))
    if fmt == "e4m3":
        words = by_word.astype(ml_dtypes.float8_e4m3fn).view(np.uint8)
    else:
        c = by_word.astype(ml_dtypes.float4_e2m1fn).view(np.uint8) & 0xF
        words = (c[..., 0::2] | (c[..., 1::2] << 4)).reshape(k // 512, 128, 2 * n)
    return np.ascontiguousarray(words), np.ascontiguousarray(byte.astype(np.uint8).reshape(k // 512, 16, n))


def unpack_weight(words, scales, fmt):
    g, _, n = scales.shape
    words = np.ascontiguousarray(words).reshape(g, 128, n, -1)
    if fmt == "e4m3":
        vals = words.view(ml_dtypes.float8_e4m3fn).astype(np.float64)
    else:
        nib = np.empty((g, 128, n, 4), np.uint8)
        nib[..., 0::2] = words & 0xF
        nib[..., 1::2] = words >> 4
        vals = E2M1[nib]
    vals = vals * np.repeat(np.exp2(scales.astype(np.float64) - 127.0), 8, axis=1)[..., None]
    return vals.transpose(0, 1, 3, 2).reshape(g * 512, n)


K, N, T, J = 512, 512, 4096, 2048


def setup_inputs():
    n = np.random.standard_normal
    s = mx_kscale(K)[:, None]
    p_tab = pack_weight(n((K, T)) * s, "e4m3")
    p_tab2 = pack_weight(n((K, T)) * s, "e4m3")
    p_wi = pack_weight(n((K, N)) / np.sqrt(2 * K) / s, "e2m1")
    return {
        "tab_words": p_tab[0],
        "tab_scales": p_tab[1],
        "tab2_words": p_tab2[0],
        "tab2_scales": p_tab2[1],
        "wr": (n((K, N)) / np.sqrt(2 * K) / s).astype(np.float32),
        "wi_words": p_wi[0],
        "wi_scales": p_wi[1],
        "offs": striped(np.random.permutation(T)[:J]),
    }


def reference(tab_words, tab_scales, tab2_words, tab2_scales, wr, wi_words, wi_scales, offs):
    idx = unstriped(offs)
    tab_ = unpack_weight(tab_words, tab_scales, "e4m3")[:, idx]
    tab2_ = unpack_weight(tab2_words, tab2_scales, "e4m3")[:, idx]
    wr_ = mxq(f64(wr), 0, "e4m3")
    wi_ = unpack_weight(wi_words, wi_scales, "e2m1")
    rr = wr_.T @ tab_
    ii = wi_.T @ tab2_
    zr = rr - ii
    ri = wr_.T @ tab2_ + wi_.T @ tab_
    zi = ri
    return zr, zi

@@ -1,0 +1,179 @@
+from contextlib import ExitStack
+
+import concourse.mybir as mybir
+
+K, N, T, J = 512, 512, 4096, 2048
+FLOPS = 4 * 2 * K * N * J
+
+F32 = mybir.dt.float32
+BF16 = mybir.dt.bfloat16
+I32 = mybir.dt.int32
+U32 = mybir.dt.uint32
+U16 = mybir.dt.uint16
+U8 = mybir.dt.uint8
+FP8X4 = mybir.dt.float8_e4m3fn_x4
+FP4X4 = mybir.dt.float4_e2m1fn_x4
+COPY = mybir.ActivationFunctionType.Copy
+MULT = mybir.AluOpType.mult
+
+P = 128
+PACK = 4
+ROWS = 128
+COLS = 512
+ROW_TILES = N // ROWS
+SLICES = J // COLS
+EARLY_N = 256
+LATE_N = N - EARLY_N
+EARLY_SLICES = 2
+
+
+def load_scale_rows(queue, plane, scales):
+    for r in range(4):
+        queue.dma_start(out=plane[r:P:32, :].bitcast(I32), in_=scales[0, r:16:4, :].bitcast(I32))
+
+
+def tile_list_cpxtab_none_kernel(
+    tc, tab_words, tab_scales, tab2_words, tab2_scales, wr, wi_words, wi_scales, offs, out_0, out_1
+):
+    nc = tc.nc
+    with ExitStack() as ctx:
+        keep = ctx.enter_context(tc.tile_pool(name="keep", bufs=1))
+        psum = ctx.enter_context(tc.psum_pool(name="psum", bufs=8))
+
+        offsets = keep.tile([P, J // 16], U16, name="offsets")
+        word_win = [keep.tile([P, T], U32, name="word_win%d" % a, align_bytes=64) for a in range(2)]
+        scale_win = [keep.tile([P, T], U8, name="scale_win%d" % a, align_bytes=64) for a in range(2)]
+        wi_codes = keep.tile([P, 2 * N], U8, name="wi_codes", align_bytes=64)
+        wi_plane = keep.tile([P, N], U8, name="wi_plane", align_bytes=64)
+        wr_rows = wr.rearrange("(p i) n -> p i n", i=PACK)
+        raw_early = keep.tile([P, PACK, EARLY_N], F32, name="raw_early")
+        raw_late = keep.tile([P, PACK, LATE_N], F32, name="raw_late")
+
+        nc.vector.memset(scale_win[0][:].bitcast(I32), 0)
+        nc.vector.memset(scale_win[1][:].bitcast(I32), 0)
+        nc.vector.memset(wi_plane[:].bitcast(I32), 0)
+
+        nc.sync.dma_start(offsets[:], offs)
+        nc.sync.dma_start(out=raw_early[:], in_=wr_rows[:, :, 0:EARLY_N])
+        nc.sync.dma_start(out=wi_codes[:].bitcast(I32), in_=wi_words[0].bitcast(I32))
+        for win, words in zip(word_win, (tab_words, tab2_words)):
+            nc.sync.dma_start(out=win[:].bitcast(I32), in_=words[0].rearrange("p t i -> p (t i)").bitcast(I32))
+        nc.sync.dma_start(out=raw_late[:], in_=wr_rows[:, :, EARLY_N:N])
+        load_scale_rows(nc.scalar, scale_win[0], tab_scales)
+        load_scale_rows(nc.gpsimd, scale_win[1], tab2_scales)
+        load_scale_rows(nc.gpsimd, wi_plane, wi_scales)
+
+        def quantise(rounded, width, name):
+            codes = keep.tile([P, width], U32, name=name + "_codes", align_bytes=64)
+            plane = keep.tile([P, width], U8, name=name + "_plane", align_bytes=64)
+            nc.vector.quantize_mx(out=codes[:].bitcast(FP8X4), scales=plane[:], in_=rounded[:])
+            return codes, plane
+
+        def interleaved(rounded):
+            return rounded[:].rearrange("p (n i) -> p n i", i=PACK)
+
+        def gather(dst, win, s):
+            nc.vector.tensor_copy(dst, win[:].indirect(offsets[:, s * (COLS // 16) : (s + 1) * (COLS // 16)]))
+
+        words = {}
+        planes = {}
+
+        def own_tile(a, s, dtype, name):
+            t = keep.tile([P, COLS], dtype, name="%s%d_%d" % (name, a, s), align_bytes=64)
+            return t[:]
+
+        plus_early = keep.tile([P, PACK * EARLY_N], BF16, name="plus_early", align_bytes=64)
+        minus_early = keep.tile([P, PACK * EARLY_N], BF16, name="minus_early", align_bytes=64)
+        nc.scalar.activation(interleaved(minus_early), raw_early[:].rearrange("p i n -> p n i"), COPY, scale=-1.0)
+        nc.scalar.activation(interleaved(plus_early), raw_early[:].rearrange("p i n -> p n i"), COPY)
+
+        for s in range(EARLY_SLICES):
+            planes[0, s] = own_tile(0, s, U8, "plane")
+            gather(planes[0, s], scale_win[0], s)
+        wr_minus = [quantise(minus_early, EARLY_N, "minus_early")]
+        wr_plus = [quantise(plus_early, EARLY_N, "plus_early")]
+        for s in range(EARLY_SLICES):
+            words[0, s] = own_tile(0, s, U32, "words")
+            gather(words[0, s], word_win[0], s)
+        for s in range(EARLY_SLICES):
+            planes[1, s] = own_tile(1, s, U8, "plane")
+            gather(planes[1, s], scale_win[1], s)
+        planes[0, EARLY_SLICES] = own_tile(0, EARLY_SLICES, U8, "plane")
+        gather(planes[0, EARLY_SLICES], scale_win[0], EARLY_SLICES)
+        for s in range(EARLY_SLICES):
+            words[1, s] = own_tile(1, s, U32, "words")
+            gather(words[1, s], word_win[1], s)
+
+        plus_late = keep.tile([P, PACK * LATE_N], BF16, name="plus_late", tag="late_a", align_bytes=64)
+        minus_late = keep.tile([P, PACK * LATE_N], BF16, name="minus_late", tag="late_b", align_bytes=64)
+        nc.vector.tensor_copy(interleaved(plus_late), raw_late[:].rearrange("p i n -> p n i"))
+        nc.vector.tensor_scalar(minus_late[:], plus_late[:], -1.0, None, MULT)
+        wr_plus.append(quantise(plus_late, LATE_N, "plus_late"))
+        wr_minus.append(quantise(minus_late, LATE_N, "minus_late"))
+
+        late_words = keep.tile([P, 4 * COLS], U32, name="late_words", tag="late_a", align_bytes=64)
+        late_planes = keep.tile([P, 4 * COLS], U8, name="late_planes", tag="late_b", align_bytes=64)
+        for s in range(EARLY_SLICES, SLICES):
+            for a in range(2):
+                place = slice((2 * (s - EARLY_SLICES) + a) * COLS, (2 * (s - EARLY_SLICES) + a + 1) * COLS)
+                if (a, s) not in planes:
+                    planes[a, s] = late_planes[:, place]
+                    gather(planes[a, s], scale_win[a], s)
+                words[a, s] = late_words[:, place]
+                gather(words[a, s], word_win[a], s)
+
+        def wr_operand(signed, m):
+            half, col = divmod(m * ROWS, EARLY_N)
+            codes, plane = signed[half]
+            return codes[:, col : col + ROWS].bitcast(FP8X4), plane[:, col : col + ROWS]
+
+        def wi_operand(m):
+            return (
+                wi_codes[:, 2 * m * ROWS : 2 * (m + 1) * ROWS].bitcast(FP4X4),
+                wi_plane[:, m * ROWS : (m + 1) * ROWS],
+            )
+
+        def product(part, m, s, dst, on_vector):
+            acc = psum.tile([P, COLS], F32, name="acc")
+            if part == 0:
+                weights = (wr_operand(wr_minus, m), wi_operand(m))
+            else:
+                weights = (wi_operand(m), wr_operand(wr_plus, m))
+            for a in range(2):
+                nc.tensor.matmul_mx(
+                    out=acc[:],
+                    lhsT=weights[a][0],
+                    lhsT_scale=weights[a][1],
+                    rhs=words[a, s].bitcast(FP8X4),
+                    rhs_scale=planes[a, s],
+                    start=(a == 0),
+                    stop=(a == 1),
+                )
+            sign = -1.0 if part == 0 else 1.0
+            if on_vector:
+                nc.vector.tensor_scalar(dst, acc[:], sign, None, MULT)
+            else:
+                nc.scalar.activation(dst, acc[:], COPY, scale=sign)
+
+        outs = (out_0, out_1)
+        for pair in range(SLICES // 2):
+            for m in range(ROW_TILES):
+                rows = slice(m * ROWS, (m + 1) * ROWS)
+                staged = [
+                    keep.tile([P, 2 * COLS], F32, name="staged%d_%d_%d" % (pair, m, part)) for part in range(2)
+                ]
+                if m == 0:
+                    for h in range(2):
+                        s = 2 * pair + h
+                        for part in range(2):
+                            dst = staged[part][:, h * COLS : (h + 1) * COLS]
+                            product(part, m, s, dst, False)
+                            nc.sync.dma_start(out=outs[part][rows, s * COLS : (s + 1) * COLS], in_=dst)
+                else:
+                    for part in range(2):
+                        for h in range(2):
+                            dst = staged[part][:, h * COLS : (h + 1) * COLS]
+                            product(part, m, 2 * pair + h, dst, pair == 1 and m >= 2 and h == 1)
+                        nc.sync.dma_start(
+                            out=outs[part][rows, 2 * pair * COLS : (2 * pair + 2) * COLS], in_=staged[part][:]
+                        )

@@ -27,8 +27,8 @@ LATE_N = N - EARLY_N
 EARLY_SLICES = 2
 
 
-def load_scale_rows(queue, plane, scales):
-    for r in range(4):
+def load_scale_rows(queue, plane, scales, rows):
+    for r in rows:
         queue.dma_start(out=plane[r:P:32, :].bitcast(I32), in_=scales[0, r:16:4, :].bitcast(I32))
 
 
@@ -54,14 +54,14 @@ def tile_list_cpxtab_none_kernel(
         nc.vector.memset(wi_plane[:].bitcast(I32), 0)
 
         nc.sync.dma_start(offsets[:], offs)
-        nc.sync.dma_start(out=raw_early[:], in_=wr_rows[:, :, 0:EARLY_N])
         nc.sync.dma_start(out=wi_codes[:].bitcast(I32), in_=wi_words[0].bitcast(I32))
+        load_scale_rows(nc.sync, scale_win[0], tab_scales, range(0, 2))
+        nc.sync.dma_start(out=raw_early[:], in_=wr_rows[:, :, 0:EARLY_N])
         for win, words in zip(word_win, (tab_words, tab2_words)):
             nc.sync.dma_start(out=win[:].bitcast(I32), in_=words[0].rearrange("p t i -> p (t i)").bitcast(I32))
         nc.sync.dma_start(out=raw_late[:], in_=wr_rows[:, :, EARLY_N:N])
-        load_scale_rows(nc.scalar, scale_win[0], tab_scales)
-        load_scale_rows(nc.gpsimd, scale_win[1], tab2_scales)
-        load_scale_rows(nc.gpsimd, wi_plane, wi_scales)
+        load_scale_rows(nc.scalar, scale_win[0], tab_scales, range(2, 4))
+        load_scale_rows(nc.scalar, scale_win[1], tab2_scales, range(4))
 
         def quantise(rounded, width, name):
             codes = keep.tile([P, width], U32, name=name + "_codes", align_bytes=64)
@@ -86,20 +86,17 @@ def tile_list_cpxtab_none_kernel(
         minus_early = keep.tile([P, PACK * EARLY_N], BF16, name="minus_early", align_bytes=64)
         nc.scalar.activation(interleaved(minus_early), raw_early[:].rearrange("p i n -> p n i"), COPY, scale=-1.0)
         nc.scalar.activation(interleaved(plus_early), raw_early[:].rearrange("p i n -> p n i"), COPY)
+        load_scale_rows(nc.scalar, wi_plane, wi_scales, range(4))
 
-        for s in range(EARLY_SLICES):
-            planes[0, s] = own_tile(0, s, U8, "plane")
-            gather(planes[0, s], scale_win[0], s)
+        for a in range(2):
+            for s in range(EARLY_SLICES + 1):
+                planes[a, s] = own_tile(a, s, U8, "plane")
+                gather(planes[a, s], scale_win[a], s)
         wr_minus = [quantise(minus_early, EARLY_N, "minus_early")]
         wr_plus = [quantise(plus_early, EARLY_N, "plus_early")]
         for s in range(EARLY_SLICES):
             words[0, s] = own_tile(0, s, U32, "words")
             gather(words[0, s], word_win[0], s)
-        for s in range(EARLY_SLICES):
-            planes[1, s] = own_tile(1, s, U8, "plane")
-            gather(planes[1, s], scale_win[1], s)
-        planes[0, EARLY_SLICES] = own_tile(0, EARLY_SLICES, U8, "plane")
-        gather(planes[0, EARLY_SLICES], scale_win[0], EARLY_SLICES)
         for s in range(EARLY_SLICES):
             words[1, s] = own_tile(1, s, U32, "words")
             gather(words[1, s], word_win[1], s)

@@ -50,18 +50,24 @@ def tile_list_cpxtab_none_kernel(
         raw_late = keep.tile([P, PACK, LATE_N], F32, name="raw_late")
 
         nc.vector.memset(scale_win[0][:].bitcast(I32), 0)
-        nc.vector.memset(scale_win[1][:].bitcast(I32), 0)
         nc.vector.memset(wi_plane[:].bitcast(I32), 0)
+        nc.vector.memset(scale_win[1][:].bitcast(I32), 0)
+
+        def load_words(a, table_words):
+            nc.sync.dma_start(
+                out=word_win[a][:].bitcast(I32), in_=table_words[0].rearrange("p t i -> p (t i)").bitcast(I32)
+            )
 
         nc.sync.dma_start(offsets[:], offs)
         nc.sync.dma_start(out=wi_codes[:].bitcast(I32), in_=wi_words[0].bitcast(I32))
-        load_scale_rows(nc.sync, scale_win[0], tab_scales, range(0, 2))
         nc.sync.dma_start(out=raw_early[:], in_=wr_rows[:, :, 0:EARLY_N])
-        for win, words in zip(word_win, (tab_words, tab2_words)):
-            nc.sync.dma_start(out=win[:].bitcast(I32), in_=words[0].rearrange("p t i -> p (t i)").bitcast(I32))
+        load_scale_rows(nc.sync, scale_win[0], tab_scales, range(4))
+        load_scale_rows(nc.sync, wi_plane, wi_scales, range(0, 2))
+        load_words(0, tab_words)
+        load_scale_rows(nc.sync, wi_plane, wi_scales, range(2, 4))
+        load_scale_rows(nc.sync, scale_win[1], tab2_scales, range(4))
+        load_words(1, tab2_words)
         nc.sync.dma_start(out=raw_late[:], in_=wr_rows[:, :, EARLY_N:N])
-        load_scale_rows(nc.scalar, scale_win[0], tab_scales, range(2, 4))
-        load_scale_rows(nc.scalar, scale_win[1], tab2_scales, range(4))
 
         def quantise(rounded, width, name):
             codes = keep.tile([P, width], U32, name=name + "_codes", align_bytes=64)
@@ -85,18 +91,19 @@ def tile_list_cpxtab_none_kernel(
         plus_early = keep.tile([P, PACK * EARLY_N], BF16, name="plus_early", align_bytes=64)
         minus_early = keep.tile([P, PACK * EARLY_N], BF16, name="minus_early", align_bytes=64)
         nc.scalar.activation(interleaved(minus_early), raw_early[:].rearrange("p i n -> p n i"), COPY, scale=-1.0)
-        nc.scalar.activation(interleaved(plus_early), raw_early[:].rearrange("p i n -> p n i"), COPY)
-        load_scale_rows(nc.scalar, wi_plane, wi_scales, range(4))
-
-        for a in range(2):
-            for s in range(EARLY_SLICES + 1):
-                planes[a, s] = own_tile(a, s, U8, "plane")
-                gather(planes[a, s], scale_win[a], s)
-        wr_minus = [quantise(minus_early, EARLY_N, "minus_early")]
+        nc.vector.tensor_copy(interleaved(plus_early), raw_early[:].rearrange("p i n -> p n i"))
         wr_plus = [quantise(plus_early, EARLY_N, "plus_early")]
+        wr_minus = [quantise(minus_early, EARLY_N, "minus_early")]
+
+        for s in range(EARLY_SLICES + 1):
+            planes[0, s] = own_tile(0, s, U8, "plane")
+            gather(planes[0, s], scale_win[0], s)
         for s in range(EARLY_SLICES):
             words[0, s] = own_tile(0, s, U32, "words")
             gather(words[0, s], word_win[0], s)
+        for s in range(EARLY_SLICES):
+            planes[1, s] = own_tile(1, s, U8, "plane")
+            gather(planes[1, s], scale_win[1], s)
         for s in range(EARLY_SLICES):
             words[1, s] = own_tile(1, s, U32, "words")
             gather(words[1, s], word_win[1], s)
@@ -153,24 +160,25 @@ def tile_list_cpxtab_none_kernel(
                 nc.scalar.activation(dst, acc[:], COPY, scale=sign)
 
         outs = (out_0, out_1)
-        for pair in range(SLICES // 2):
+
+        def staging(name, width):
+            return keep.tile([P, width], F32, name=name)
+
+        def single(part, m, s, on_vector):
+            staged = staging("staged%d_%d_%d" % (s, m, part), COLS)
+            product(part, m, s, staged[:], on_vector)
+            nc.sync.dma_start(out=outs[part][m * ROWS : (m + 1) * ROWS, s * COLS : (s + 1) * COLS], in_=staged[:])
+
+        for s in range(EARLY_SLICES):
+            for part in range(2):
+                single(part, 0, s, False)
+        for m in range(1, ROW_TILES):
+            for part in range(2):
+                staged = staging("paired%d_%d" % (m, part), EARLY_SLICES * COLS)
+                for s in range(EARLY_SLICES):
+                    product(part, m, s, staged[:, s * COLS : (s + 1) * COLS], False)
+                nc.sync.dma_start(out=outs[part][m * ROWS : (m + 1) * ROWS, 0 : EARLY_SLICES * COLS], in_=staged[:])
+        for s in range(EARLY_SLICES, SLICES):
             for m in range(ROW_TILES):
-                rows = slice(m * ROWS, (m + 1) * ROWS)
-                staged = [
-                    keep.tile([P, 2 * COLS], F32, name="staged%d_%d_%d" % (pair, m, part)) for part in range(2)
-                ]
-                if m == 0:
-                    for h in range(2):
-                        s = 2 * pair + h
-                        for part in range(2):
-                            dst = staged[part][:, h * COLS : (h + 1) * COLS]
-                            product(part, m, s, dst, False)
-                            nc.sync.dma_start(out=outs[part][rows, s * COLS : (s + 1) * COLS], in_=dst)
-                else:
-                    for part in range(2):
-                        for h in range(2):
-                            dst = staged[part][:, h * COLS : (h + 1) * COLS]
-                            product(part, m, 2 * pair + h, dst, pair == 1 and m >= 2 and h == 1)
-                        nc.sync.dma_start(
-                            out=outs[part][rows, 2 * pair * COLS : (2 * pair + 2) * COLS], in_=staged[part][:]
-                        )
+                for part in range(2):
+                    single(part, m, s, part == 1 and (s == SLICES - 1 or m >= 2))

@@ -24,12 +24,6 @@ ROW_TILES = N // ROWS
 SLICES = J // COLS
 EARLY_N = 256
 LATE_N = N - EARLY_N
-EARLY_SLICES = 2
-
-
-def load_scale_rows(queue, plane, scales, rows):
-    for r in rows:
-        queue.dma_start(out=plane[r:P:32, :].bitcast(I32), in_=scales[0, r:16:4, :].bitcast(I32))
 
 
 def tile_list_cpxtab_none_kernel(
@@ -42,35 +36,31 @@ def tile_list_cpxtab_none_kernel(
 
         offsets = keep.tile([P, J // 16], U16, name="offsets")
         word_win = [keep.tile([P, T], U32, name="word_win%d" % a, align_bytes=64) for a in range(2)]
-        scale_win = [keep.tile([P, T], U8, name="scale_win%d" % a, align_bytes=64) for a in range(2)]
+        scale_win = [keep.tile([P, T], U8, name="scale_win%d" % a, tag="scale_win%d" % a, align_bytes=64) for a in range(2)]
         wi_codes = keep.tile([P, 2 * N], U8, name="wi_codes", align_bytes=64)
         wi_plane = keep.tile([P, N], U8, name="wi_plane", align_bytes=64)
         wr_rows = wr.rearrange("(p i) n -> p i n", i=PACK)
         raw_early = keep.tile([P, PACK, EARLY_N], F32, name="raw_early")
         raw_late = keep.tile([P, PACK, LATE_N], F32, name="raw_late")
 
-        nc.vector.memset(scale_win[0][:].bitcast(I32), 0)
-        nc.vector.memset(wi_plane[:].bitcast(I32), 0)
+        nc.vector.memset(scale_win[0][:, 0 : T // 2].bitcast(I32), 0)
+        nc.gpsimd.memset(scale_win[0][:, T // 2 : T].bitcast(I32), 0)
         nc.vector.memset(scale_win[1][:].bitcast(I32), 0)
-
-        def load_words(a, table_words):
-            nc.sync.dma_start(
-                out=word_win[a][:].bitcast(I32), in_=table_words[0].rearrange("p t i -> p (t i)").bitcast(I32)
-            )
+        nc.vector.memset(wi_plane[:].bitcast(I32), 0)
 
         nc.sync.dma_start(offsets[:], offs)
         nc.sync.dma_start(out=wi_codes[:].bitcast(I32), in_=wi_words[0].bitcast(I32))
+        for win, table_scales in zip(scale_win, (tab_scales, tab2_scales)):
+            nc.sync.dma_start(out=win[0:P:8, :].bitcast(I32), in_=table_scales[0].bitcast(I32))
         nc.sync.dma_start(out=raw_early[:], in_=wr_rows[:, :, 0:EARLY_N])
-        load_scale_rows(nc.sync, scale_win[0], tab_scales, range(4))
-        load_scale_rows(nc.sync, wi_plane, wi_scales, range(0, 2))
-        load_words(0, tab_words)
-        load_scale_rows(nc.sync, wi_plane, wi_scales, range(2, 4))
-        load_scale_rows(nc.sync, scale_win[1], tab2_scales, range(4))
-        load_words(1, tab2_words)
+        for win, table_words in zip(word_win, (tab_words, tab2_words)):
+            nc.sync.dma_start(out=win[:].bitcast(I32), in_=table_words[0].rearrange("p t i -> p (t i)").bitcast(I32))
         nc.sync.dma_start(out=raw_late[:], in_=wr_rows[:, :, EARLY_N:N])
+        for r in range(4):
+            nc.scalar.dma_start(out=wi_plane[r:P:32, :].bitcast(I32), in_=wi_scales[0, r:16:4, :].bitcast(I32))
 
-        def quantise(rounded, width, name):
-            codes = keep.tile([P, width], U32, name=name + "_codes", align_bytes=64)
+        def quantise(rounded, width, name, tag):
+            codes = keep.tile([P, width], U32, name=name + "_codes", tag=tag, align_bytes=64)
             plane = keep.tile([P, width], U8, name=name + "_plane", align_bytes=64)
             nc.vector.quantize_mx(out=codes[:].bitcast(FP8X4), scales=plane[:], in_=rounded[:])
             return codes, plane
@@ -88,42 +78,45 @@ def tile_list_cpxtab_none_kernel(
             t = keep.tile([P, COLS], dtype, name="%s%d_%d" % (name, a, s), align_bytes=64)
             return t[:]
 
-        plus_early = keep.tile([P, PACK * EARLY_N], BF16, name="plus_early", align_bytes=64)
-        minus_early = keep.tile([P, PACK * EARLY_N], BF16, name="minus_early", align_bytes=64)
-        nc.scalar.activation(interleaved(minus_early), raw_early[:].rearrange("p i n -> p n i"), COPY, scale=-1.0)
-        nc.vector.tensor_copy(interleaved(plus_early), raw_early[:].rearrange("p i n -> p n i"))
-        wr_plus = [quantise(plus_early, EARLY_N, "plus_early")]
-        wr_minus = [quantise(minus_early, EARLY_N, "minus_early")]
+        both_early = keep.tile([P, 2 * PACK * EARLY_N], BF16, name="both_early", align_bytes=64)
+        for half, sign in enumerate((-1.0, 1.0)):
+            dst = both_early[:, half * PACK * EARLY_N : (half + 1) * PACK * EARLY_N]
+            nc.scalar.activation(
+                dst.rearrange("p (n i) -> p n i", i=PACK), raw_early[:].rearrange("p i n -> p n i"), COPY, scale=sign
+            )
 
-        for s in range(EARLY_SLICES + 1):
-            planes[0, s] = own_tile(0, s, U8, "plane")
-            gather(planes[0, s], scale_win[0], s)
-        for s in range(EARLY_SLICES):
-            words[0, s] = own_tile(0, s, U32, "words")
-            gather(words[0, s], word_win[0], s)
-        for s in range(EARLY_SLICES):
-            planes[1, s] = own_tile(1, s, U8, "plane")
-            gather(planes[1, s], scale_win[1], s)
-        for s in range(EARLY_SLICES):
-            words[1, s] = own_tile(1, s, U32, "words")
-            gather(words[1, s], word_win[1], s)
+        for a in range(2):
+            spread = keep.tile([P, J], U8, name="spread%d" % a, align_bytes=64)
+            nc.vector.tensor_copy(spread[:], scale_win[a][:].indirect(offsets[:]))
+            plane = keep.tile([P, J], U8, name="plane%d" % a, align_bytes=64)
+            nc.vector.tensor_copy(plane[:].bitcast(I32), spread[:].bitcast(I32))
+            for r in range(1, 4):
+                nc.scalar.dma_start(out=plane[r:P:32, :].bitcast(I32), in_=spread[8 * r : P : 32, :].bitcast(I32))
+            for s in range(SLICES):
+                planes[a, s] = plane[:, s * COLS : (s + 1) * COLS]
+        codes, plane = quantise(both_early, 2 * EARLY_N, "early", "early_codes")
+        wr_minus = [(codes[:, 0:EARLY_N], plane[:, 0:EARLY_N])]
+        wr_plus = [(codes[:, EARLY_N:], plane[:, EARLY_N:])]
+        for a in range(2):
+            words[a, 0] = own_tile(a, 0, U32, "words")
+            gather(words[a, 0], word_win[a], 0)
 
         plus_late = keep.tile([P, PACK * LATE_N], BF16, name="plus_late", tag="late_a", align_bytes=64)
         minus_late = keep.tile([P, PACK * LATE_N], BF16, name="minus_late", tag="late_b", align_bytes=64)
         nc.vector.tensor_copy(interleaved(plus_late), raw_late[:].rearrange("p i n -> p n i"))
         nc.vector.tensor_scalar(minus_late[:], plus_late[:], -1.0, None, MULT)
-        wr_plus.append(quantise(plus_late, LATE_N, "plus_late"))
-        wr_minus.append(quantise(minus_late, LATE_N, "minus_late"))
+        codes, plane = quantise(plus_late, LATE_N, "plus_late", "plus_late_codes")
+        wr_plus.append((codes[:], plane[:]))
+        codes, plane = quantise(minus_late, LATE_N, "minus_late", "minus_late_codes")
+        wr_minus.append((codes[:], plane[:]))
 
-        late_words = keep.tile([P, 4 * COLS], U32, name="late_words", tag="late_a", align_bytes=64)
-        late_planes = keep.tile([P, 4 * COLS], U8, name="late_planes", tag="late_b", align_bytes=64)
-        for s in range(EARLY_SLICES, SLICES):
+        late_words = [
+            keep.tile([P, J - COLS], U32, name="late_words%d" % a, tag=tag, align_bytes=64)
+            for a, tag in enumerate(("late_a", "late_b"))
+        ]
+        for s in range(1, SLICES):
             for a in range(2):
-                place = slice((2 * (s - EARLY_SLICES) + a) * COLS, (2 * (s - EARLY_SLICES) + a + 1) * COLS)
-                if (a, s) not in planes:
-                    planes[a, s] = late_planes[:, place]
-                    gather(planes[a, s], scale_win[a], s)
-                words[a, s] = late_words[:, place]
+                words[a, s] = late_words[a][:, (s - 1) * COLS : s * COLS]
                 gather(words[a, s], word_win[a], s)
 
         def wr_operand(signed, m):
@@ -143,15 +136,16 @@ def tile_list_cpxtab_none_kernel(
                 weights = (wr_operand(wr_minus, m), wi_operand(m))
             else:
                 weights = (wi_operand(m), wr_operand(wr_plus, m))
-            for a in range(2):
+            order = (0, 1) if (m, s) == (0, 0) else (1, 0)
+            for a in order:
                 nc.tensor.matmul_mx(
                     out=acc[:],
                     lhsT=weights[a][0],
                     lhsT_scale=weights[a][1],
                     rhs=words[a, s].bitcast(FP8X4),
                     rhs_scale=planes[a, s],
-                    start=(a == 0),
-                    stop=(a == 1),
+                    start=(a == order[0]),
+                    stop=(a == order[1]),
                 )
             sign = -1.0 if part == 0 else 1.0
             if on_vector:
@@ -169,16 +163,13 @@ def tile_list_cpxtab_none_kernel(
             product(part, m, s, staged[:], on_vector)
             nc.sync.dma_start(out=outs[part][m * ROWS : (m + 1) * ROWS, s * COLS : (s + 1) * COLS], in_=staged[:])
 
-        for s in range(EARLY_SLICES):
-            for part in range(2):
-                single(part, 0, s, False)
-        for m in range(1, ROW_TILES):
-            for part in range(2):
-                staged = staging("paired%d_%d" % (m, part), EARLY_SLICES * COLS)
-                for s in range(EARLY_SLICES):
-                    product(part, m, s, staged[:, s * COLS : (s + 1) * COLS], False)
-                nc.sync.dma_start(out=outs[part][m * ROWS : (m + 1) * ROWS, 0 : EARLY_SLICES * COLS], in_=staged[:])
-        for s in range(EARLY_SLICES, SLICES):
+        for s in range(2):
             for m in range(ROW_TILES):
                 for part in range(2):
-                    single(part, m, s, part == 1 and (s == SLICES - 1 or m >= 2))
+                    single(part, m, s, False)
+        for m in range(ROW_TILES):
+            for part in range(2):
+                staged = staging("paired%d_%d" % (m, part), 2 * COLS)
+                for u in range(2):
+                    product(part, m, 2 + u, staged[:, u * COLS : (u + 1) * COLS], u == 1)
+                nc.sync.dma_start(out=outs[part][m * ROWS : (m + 1) * ROWS, 2 * COLS : J], in_=staged[:])

@@ -24,6 +24,7 @@ ROW_TILES = N // ROWS
 SLICES = J // COLS
 EARLY_N = 256
 LATE_N = N - EARLY_N
+AHEAD = 3
 
 
 def tile_list_cpxtab_none_kernel(
@@ -36,31 +37,38 @@ def tile_list_cpxtab_none_kernel(
 
         offsets = keep.tile([P, J // 16], U16, name="offsets")
         word_win = [keep.tile([P, T], U32, name="word_win%d" % a, align_bytes=64) for a in range(2)]
-        scale_win = [keep.tile([P, T], U8, name="scale_win%d" % a, tag="scale_win%d" % a, align_bytes=64) for a in range(2)]
+        scale_win = [keep.tile([P, T], U8, name="scale_win%d" % a, align_bytes=64) for a in range(2)]
+        late_win = [keep.tile([P, T], U8, name="late_win%d" % a, tag="late_win%d" % a, align_bytes=64) for a in range(2)]
         wi_codes = keep.tile([P, 2 * N], U8, name="wi_codes", align_bytes=64)
-        wi_plane = keep.tile([P, N], U8, name="wi_plane", align_bytes=64)
+        wi_spread = keep.tile([P, N], U8, name="wi_spread", align_bytes=64)
         wr_rows = wr.rearrange("(p i) n -> p i n", i=PACK)
-        raw_early = keep.tile([P, PACK, EARLY_N], F32, name="raw_early")
+        raw_early = keep.tile([P, PACK, EARLY_N], F32, name="raw_early", tag="early", align_bytes=64)
         raw_late = keep.tile([P, PACK, LATE_N], F32, name="raw_late")
 
         nc.vector.memset(scale_win[0][:, 0 : T // 2].bitcast(I32), 0)
         nc.gpsimd.memset(scale_win[0][:, T // 2 : T].bitcast(I32), 0)
         nc.vector.memset(scale_win[1][:].bitcast(I32), 0)
-        nc.vector.memset(wi_plane[:].bitcast(I32), 0)
+        nc.vector.memset(wi_spread[:].bitcast(I32), 0)
+        for win in late_win:
+            nc.vector.memset(win[:].bitcast(I32), 0)
 
         nc.sync.dma_start(offsets[:], offs)
-        nc.sync.dma_start(out=wi_codes[:].bitcast(I32), in_=wi_words[0].bitcast(I32))
+        nc.sync.dma_start(out=raw_early[:], in_=wr_rows[:, :, 0:EARLY_N])
         for win, table_scales in zip(scale_win, (tab_scales, tab2_scales)):
             nc.sync.dma_start(out=win[0:P:8, :].bitcast(I32), in_=table_scales[0].bitcast(I32))
-        nc.sync.dma_start(out=raw_early[:], in_=wr_rows[:, :, 0:EARLY_N])
+        nc.sync.dma_start(out=wi_codes[:].bitcast(I32), in_=wi_words[0].bitcast(I32))
+        nc.sync.dma_start(out=wi_spread[0:P:8, :].bitcast(I32), in_=wi_scales[0].bitcast(I32))
         for win, table_words in zip(word_win, (tab_words, tab2_words)):
             nc.sync.dma_start(out=win[:].bitcast(I32), in_=table_words[0].rearrange("p t i -> p (t i)").bitcast(I32))
         nc.sync.dma_start(out=raw_late[:], in_=wr_rows[:, :, EARLY_N:N])
-        for r in range(4):
-            nc.scalar.dma_start(out=wi_plane[r:P:32, :].bitcast(I32), in_=wi_scales[0, r:16:4, :].bitcast(I32))
+        for win, table_scales in zip(late_win, (tab_scales, tab2_scales)):
+            for q in range(4):
+                nc.sync.dma_start(
+                    out=win[32 * q : 32 * q + 4, :].bitcast(I32), in_=table_scales[0, 4 * q : 4 * q + 4, :].bitcast(I32)
+                )
 
-        def quantise(rounded, width, name, tag):
-            codes = keep.tile([P, width], U32, name=name + "_codes", tag=tag, align_bytes=64)
+        def quantise(rounded, width, name):
+            codes = keep.tile([P, width], U32, name=name + "_codes", align_bytes=64)
             plane = keep.tile([P, width], U8, name=name + "_plane", align_bytes=64)
             nc.vector.quantize_mx(out=codes[:].bitcast(FP8X4), scales=plane[:], in_=rounded[:])
             return codes, plane
@@ -68,14 +76,22 @@ def tile_list_cpxtab_none_kernel(
         def interleaved(rounded):
             return rounded[:].rearrange("p (n i) -> p n i", i=PACK)
 
-        def gather(dst, win, s):
-            nc.vector.tensor_copy(dst, win[:].indirect(offsets[:, s * (COLS // 16) : (s + 1) * (COLS // 16)]))
+        def gather(dst, win, s, count=1):
+            nc.vector.tensor_copy(dst, win[:].indirect(offsets[:, s * (COLS // 16) : (s + count) * (COLS // 16)]))
+
+        def carry_rows(queue, tile):
+            for r in range(1, 4):
+                queue.dma_start(out=tile[r:P:32, :].bitcast(I32), in_=tile[8 * r : P : 32, :].bitcast(I32))
 
         words = {}
         planes = {}
 
-        def own_tile(a, s, dtype, name):
-            t = keep.tile([P, COLS], dtype, name="%s%d_%d" % (name, a, s), align_bytes=64)
+        def gather_words(a, s, dst):
+            words[a, s] = dst
+            gather(dst, word_win[a], s)
+
+        def own_words(a, s):
+            t = keep.tile([P, COLS], U32, name="words%d_%d" % (a, s), align_bytes=64)
             return t[:]
 
         both_early = keep.tile([P, 2 * PACK * EARLY_N], BF16, name="both_early", align_bytes=64)
@@ -85,39 +101,47 @@ def tile_list_cpxtab_none_kernel(
                 dst.rearrange("p (n i) -> p n i", i=PACK), raw_early[:].rearrange("p i n -> p n i"), COPY, scale=sign
             )
 
+        half_j = J // 2
+        spread = keep.tile([P, J], U8, name="spread", align_bytes=64)
         for a in range(2):
-            spread = keep.tile([P, J], U8, name="spread%d" % a, align_bytes=64)
-            nc.vector.tensor_copy(spread[:], scale_win[a][:].indirect(offsets[:]))
-            plane = keep.tile([P, J], U8, name="plane%d" % a, align_bytes=64)
-            nc.vector.tensor_copy(plane[:].bitcast(I32), spread[:].bitcast(I32))
-            for r in range(1, 4):
-                nc.scalar.dma_start(out=plane[r:P:32, :].bitcast(I32), in_=spread[8 * r : P : 32, :].bitcast(I32))
-            for s in range(SLICES):
-                planes[a, s] = plane[:, s * COLS : (s + 1) * COLS]
-        codes, plane = quantise(both_early, 2 * EARLY_N, "early", "early_codes")
+            gather(spread[:, a * half_j : (a + 1) * half_j], scale_win[a], 0, 2)
+        first_planes = keep.tile([P, J + N], U8, name="first_planes", tag="early", align_bytes=64)
+        nc.vector.tensor_copy(first_planes[:, 0:J].bitcast(I32), spread[:].bitcast(I32))
+        nc.vector.tensor_copy(first_planes[:, J:].bitcast(I32), wi_spread[:].bitcast(I32))
+        carry_rows(nc.scalar, first_planes)
+        wi_plane = first_planes[:, J:]
+        for a in range(2):
+            for s in range(2):
+                planes[a, s] = first_planes[:, a * half_j + s * COLS : a * half_j + (s + 1) * COLS]
+
+        codes, plane = quantise(both_early, 2 * EARLY_N, "early")
         wr_minus = [(codes[:, 0:EARLY_N], plane[:, 0:EARLY_N])]
         wr_plus = [(codes[:, EARLY_N:], plane[:, EARLY_N:])]
-        for a in range(2):
-            words[a, 0] = own_tile(a, 0, U32, "words")
-            gather(words[a, 0], word_win[a], 0)
+        for s in range(AHEAD):
+            gather_words(0, s, own_words(0, s))
+        for s in range(2):
+            gather_words(1, s, own_words(1, s))
 
         plus_late = keep.tile([P, PACK * LATE_N], BF16, name="plus_late", tag="late_a", align_bytes=64)
         minus_late = keep.tile([P, PACK * LATE_N], BF16, name="minus_late", tag="late_b", align_bytes=64)
         nc.vector.tensor_copy(interleaved(plus_late), raw_late[:].rearrange("p i n -> p n i"))
         nc.vector.tensor_scalar(minus_late[:], plus_late[:], -1.0, None, MULT)
-        codes, plane = quantise(plus_late, LATE_N, "plus_late", "plus_late_codes")
+        codes, plane = quantise(plus_late, LATE_N, "plus_late")
         wr_plus.append((codes[:], plane[:]))
-        codes, plane = quantise(minus_late, LATE_N, "minus_late", "minus_late_codes")
+        codes, plane = quantise(minus_late, LATE_N, "minus_late")
         wr_minus.append((codes[:], plane[:]))
 
-        late_words = [
-            keep.tile([P, J - COLS], U32, name="late_words%d" % a, tag=tag, align_bytes=64)
-            for a, tag in enumerate(("late_a", "late_b"))
-        ]
-        for s in range(1, SLICES):
-            for a in range(2):
-                words[a, s] = late_words[a][:, (s - 1) * COLS : s * COLS]
-                gather(words[a, s], word_win[a], s)
+        third_words = keep.tile([P, COLS], U32, name="third_words", tag="late_a", align_bytes=64)
+        late_planes = keep.tile([P, 4 * COLS], U8, name="late_planes", tag="late_b", align_bytes=64)
+        gather_words(1, 2, third_words[:])
+        gather(late_planes[:, 0 : 2 * COLS], late_win[0], 2, 2)
+        for s in range(2, SLICES):
+            planes[0, s] = late_planes[:, (s - 2) * COLS : (s - 1) * COLS]
+            planes[1, s] = late_planes[:, s * COLS : (s + 1) * COLS]
+            gather(planes[1, s], late_win[1], s)
+        last_words = keep.tile([P, 2 * COLS], U32, name="last_words", tag="late_win1", align_bytes=64)
+        for a in range(2):
+            gather_words(a, 3, last_words[:, a * COLS : (a + 1) * COLS])
 
         def wr_operand(signed, m):
             half, col = divmod(m * ROWS, EARLY_N)
@@ -136,7 +160,7 @@ def tile_list_cpxtab_none_kernel(
                 weights = (wr_operand(wr_minus, m), wi_operand(m))
             else:
                 weights = (wi_operand(m), wr_operand(wr_plus, m))
-            order = (0, 1) if (m, s) == (0, 0) else (1, 0)
+            order = (0, 1) if s == 0 and m < 2 else (1, 0)
             for a in order:
                 nc.tensor.matmul_mx(
                     out=acc[:],
@@ -163,13 +187,21 @@ def tile_list_cpxtab_none_kernel(
             product(part, m, s, staged[:], on_vector)
             nc.sync.dma_start(out=outs[part][m * ROWS : (m + 1) * ROWS, s * COLS : (s + 1) * COLS], in_=staged[:])
 
+        def paired(part, m, s0, vector_too):
+            staged = staging("paired%d_%d_%d" % (s0, m, part), 2 * COLS)
+            for u in range(2):
+                product(part, m, s0 + u, staged[:, u * COLS : (u + 1) * COLS], vector_too and u == 1)
+            nc.sync.dma_start(
+                out=outs[part][m * ROWS : (m + 1) * ROWS, s0 * COLS : (s0 + 2) * COLS], in_=staged[:]
+            )
+
         for s in range(2):
-            for m in range(ROW_TILES):
+            for m in range(2):
                 for part in range(2):
                     single(part, m, s, False)
+        for m in range(2, ROW_TILES):
+            for part in range(2):
+                paired(part, m, 0, False)
         for m in range(ROW_TILES):
             for part in range(2):
-                staged = staging("paired%d_%d" % (m, part), 2 * COLS)
-                for u in range(2):
-                    product(part, m, 2 + u, staged[:, u * COLS : (u + 1) * COLS], u == 1)
-                nc.sync.dma_start(out=outs[part][m * ROWS : (m + 1) * ROWS, 2 * COLS : J], in_=staged[:])
+                paired(part, m, 2, True)

@@ -37,8 +37,7 @@ def tile_list_cpxtab_none_kernel(
 
         offsets = keep.tile([P, J // 16], U16, name="offsets")
         word_win = [keep.tile([P, T], U32, name="word_win%d" % a, align_bytes=64) for a in range(2)]
-        scale_win = [keep.tile([P, T], U8, name="scale_win%d" % a, align_bytes=64) for a in range(2)]
-        late_win = [keep.tile([P, T], U8, name="late_win%d" % a, tag="late_win%d" % a, align_bytes=64) for a in range(2)]
+        scale_win = [keep.tile([P, T], U8, name="scale_win%d" % a, tag="scale_win%d" % a, align_bytes=64) for a in range(2)]
         wi_codes = keep.tile([P, 2 * N], U8, name="wi_codes", align_bytes=64)
         wi_spread = keep.tile([P, N], U8, name="wi_spread", align_bytes=64)
         wr_rows = wr.rearrange("(p i) n -> p i n", i=PACK)
@@ -49,8 +48,6 @@ def tile_list_cpxtab_none_kernel(
         nc.gpsimd.memset(scale_win[0][:, T // 2 : T].bitcast(I32), 0)
         nc.vector.memset(scale_win[1][:].bitcast(I32), 0)
         nc.vector.memset(wi_spread[:].bitcast(I32), 0)
-        for win in late_win:
-            nc.vector.memset(win[:].bitcast(I32), 0)
 
         nc.sync.dma_start(offsets[:], offs)
         nc.sync.dma_start(out=raw_early[:], in_=wr_rows[:, :, 0:EARLY_N])
@@ -61,11 +58,6 @@ def tile_list_cpxtab_none_kernel(
         for win, table_words in zip(word_win, (tab_words, tab2_words)):
             nc.sync.dma_start(out=win[:].bitcast(I32), in_=table_words[0].rearrange("p t i -> p (t i)").bitcast(I32))
         nc.sync.dma_start(out=raw_late[:], in_=wr_rows[:, :, EARLY_N:N])
-        for win, table_scales in zip(late_win, (tab_scales, tab2_scales)):
-            for q in range(4):
-                nc.sync.dma_start(
-                    out=win[32 * q : 32 * q + 4, :].bitcast(I32), in_=table_scales[0, 4 * q : 4 * q + 4, :].bitcast(I32)
-                )
 
         def quantise(rounded, width, name):
             codes = keep.tile([P, width], U32, name=name + "_codes", align_bytes=64)
@@ -110,6 +102,9 @@ def tile_list_cpxtab_none_kernel(
         nc.vector.tensor_copy(first_planes[:, J:].bitcast(I32), wi_spread[:].bitcast(I32))
         carry_rows(nc.scalar, first_planes)
         wi_plane = first_planes[:, J:]
+        for win, table_scales in zip(scale_win, (tab_scales, tab2_scales)):
+            for r in range(1, 4):
+                nc.sync.dma_start(out=win[r:P:32, :].bitcast(I32), in_=table_scales[0, r:16:4, :].bitcast(I32))
         for a in range(2):
             for s in range(2):
                 planes[a, s] = first_planes[:, a * half_j + s * COLS : a * half_j + (s + 1) * COLS]
@@ -134,12 +129,12 @@ def tile_list_cpxtab_none_kernel(
         third_words = keep.tile([P, COLS], U32, name="third_words", tag="late_a", align_bytes=64)
         late_planes = keep.tile([P, 4 * COLS], U8, name="late_planes", tag="late_b", align_bytes=64)
         gather_words(1, 2, third_words[:])
-        gather(late_planes[:, 0 : 2 * COLS], late_win[0], 2, 2)
+        gather(late_planes[:, 0 : 2 * COLS], scale_win[0], 2, 2)
         for s in range(2, SLICES):
             planes[0, s] = late_planes[:, (s - 2) * COLS : (s - 1) * COLS]
             planes[1, s] = late_planes[:, s * COLS : (s + 1) * COLS]
-            gather(planes[1, s], late_win[1], s)
-        last_words = keep.tile([P, 2 * COLS], U32, name="last_words", tag="late_win1", align_bytes=64)
+            gather(planes[1, s], scale_win[1], s)
+        last_words = keep.tile([P, 2 * COLS], U32, name="last_words", tag="scale_win1", align_bytes=64)
         for a in range(2):
             gather_words(a, 3, last_words[:, a * COLS : (a + 1) * COLS])
 

@@ -42,22 +42,24 @@ def tile_list_cpxtab_none_kernel(
         wi_spread = keep.tile([P, N], U8, name="wi_spread", align_bytes=64)
         wr_rows = wr.rearrange("(p i) n -> p i n", i=PACK)
         raw_early = keep.tile([P, PACK, EARLY_N], F32, name="raw_early", tag="early", align_bytes=64)
-        raw_late = keep.tile([P, PACK, LATE_N], F32, name="raw_late")
 
         nc.vector.memset(scale_win[0][:, 0 : T // 2].bitcast(I32), 0)
         nc.gpsimd.memset(scale_win[0][:, T // 2 : T].bitcast(I32), 0)
-        nc.vector.memset(scale_win[1][:].bitcast(I32), 0)
         nc.vector.memset(wi_spread[:].bitcast(I32), 0)
+        nc.vector.memset(scale_win[1][:].bitcast(I32), 0)
+
+        def load_words(a, table_words):
+            nc.sync.dma_start(
+                out=word_win[a][:].bitcast(I32), in_=table_words[0].rearrange("p t i -> p (t i)").bitcast(I32)
+            )
 
         nc.sync.dma_start(offsets[:], offs)
-        nc.sync.dma_start(out=raw_early[:], in_=wr_rows[:, :, 0:EARLY_N])
-        for win, table_scales in zip(scale_win, (tab_scales, tab2_scales)):
-            nc.sync.dma_start(out=win[0:P:8, :].bitcast(I32), in_=table_scales[0].bitcast(I32))
         nc.sync.dma_start(out=wi_codes[:].bitcast(I32), in_=wi_words[0].bitcast(I32))
+        nc.sync.dma_start(out=scale_win[0][0:P:8, :].bitcast(I32), in_=tab_scales[0].bitcast(I32))
         nc.sync.dma_start(out=wi_spread[0:P:8, :].bitcast(I32), in_=wi_scales[0].bitcast(I32))
-        for win, table_words in zip(word_win, (tab_words, tab2_words)):
-            nc.sync.dma_start(out=win[:].bitcast(I32), in_=table_words[0].rearrange("p t i -> p (t i)").bitcast(I32))
-        nc.sync.dma_start(out=raw_late[:], in_=wr_rows[:, :, EARLY_N:N])
+        nc.sync.dma_start(out=raw_early[:], in_=wr_rows[:, :, 0:EARLY_N])
+        nc.sync.dma_start(out=scale_win[1][0:P:8, :].bitcast(I32), in_=tab2_scales[0].bitcast(I32))
+        load_words(0, tab_words)
 
         def quantise(rounded, width, name):
             codes = keep.tile([P, width], U32, name=name + "_codes", align_bytes=64)
@@ -94,20 +96,27 @@ def tile_list_cpxtab_none_kernel(
             )
 
         half_j = J // 2
-        spread = keep.tile([P, J], U8, name="spread", align_bytes=64)
+        first_planes = []
         for a in range(2):
-            gather(spread[:, a * half_j : (a + 1) * half_j], scale_win[a], 0, 2)
-        first_planes = keep.tile([P, J + N], U8, name="first_planes", tag="early", align_bytes=64)
-        nc.vector.tensor_copy(first_planes[:, 0:J].bitcast(I32), spread[:].bitcast(I32))
-        nc.vector.tensor_copy(first_planes[:, J:].bitcast(I32), wi_spread[:].bitcast(I32))
-        carry_rows(nc.scalar, first_planes)
-        wi_plane = first_planes[:, J:]
+            spread = keep.tile([P, half_j], U8, name="spread%d" % a, align_bytes=64)
+            gather(spread[:], scale_win[a], 0, 2)
+            made = keep.tile([P, half_j + (N if a == 0 else 0)], U8, name="first_planes%d" % a, align_bytes=64)
+            nc.vector.tensor_copy(made[:, 0:half_j].bitcast(I32), spread[:].bitcast(I32))
+            if a == 0:
+                nc.vector.tensor_copy(made[:, half_j:].bitcast(I32), wi_spread[:].bitcast(I32))
+            carry_rows(nc.sync, made)
+            if a == 0:
+                load_words(1, tab2_words)
+            first_planes.append(made)
+        raw_late = keep.tile([P, PACK, LATE_N], F32, name="raw_late")
+        nc.sync.dma_start(out=raw_late[:], in_=wr_rows[:, :, EARLY_N:N])
+        wi_plane = first_planes[0][:, half_j:]
         for win, table_scales in zip(scale_win, (tab_scales, tab2_scales)):
             for r in range(1, 4):
                 nc.sync.dma_start(out=win[r:P:32, :].bitcast(I32), in_=table_scales[0, r:16:4, :].bitcast(I32))
         for a in range(2):
             for s in range(2):
-                planes[a, s] = first_planes[:, a * half_j + s * COLS : a * half_j + (s + 1) * COLS]
+                planes[a, s] = first_planes[a][:, s * COLS : (s + 1) * COLS]
 
         codes, plane = quantise(both_early, 2 * EARLY_N, "early")
         wr_minus = [(codes[:, 0:EARLY_N], plane[:, 0:EARLY_N])]
@@ -126,9 +135,11 @@ def tile_list_cpxtab_none_kernel(
         codes, plane = quantise(minus_late, LATE_N, "minus_late")
         wr_minus.append((codes[:], plane[:]))
 
-        third_words = keep.tile([P, COLS], U32, name="third_words", tag="late_a", align_bytes=64)
+        third_words = keep.tile([P, 2 * COLS], U32, name="third_words", tag="late_a", align_bytes=64)
         late_planes = keep.tile([P, 4 * COLS], U8, name="late_planes", tag="late_b", align_bytes=64)
-        gather_words(1, 2, third_words[:])
+        for a in range(2):
+            if (a, 2) not in words:
+                gather_words(a, 2, third_words[:, a * COLS : (a + 1) * COLS])
         gather(late_planes[:, 0 : 2 * COLS], scale_win[0], 2, 2)
         for s in range(2, SLICES):
             planes[0, s] = late_planes[:, (s - 2) * COLS : (s - 1) * COLS]
@@ -155,7 +166,7 @@ def tile_list_cpxtab_none_kernel(
                 weights = (wr_operand(wr_minus, m), wi_operand(m))
             else:
                 weights = (wi_operand(m), wr_operand(wr_plus, m))
-            order = (0, 1) if s == 0 and m < 2 else (1, 0)
+            order = (0, 1) if s < 2 and m < 2 else (1, 0)
             for a in order:
                 nc.tensor.matmul_mx(
                     out=acc[:],
@@ -197,6 +208,18 @@ def tile_list_cpxtab_none_kernel(
         for m in range(2, ROW_TILES):
             for part in range(2):
                 paired(part, m, 0, False)
-        for m in range(ROW_TILES):
+        def stacked(part, m0, s):
+            staged = staging("stacked%d_%d_%d" % (s, m0, part), 2 * COLS)
+            for u in range(2):
+                product(part, m0 + u, s, staged[:, u * COLS : (u + 1) * COLS], s == SLICES - 1 and u == 0)
+            rows = outs[part][m0 * ROWS : (m0 + 2) * ROWS, s * COLS : (s + 1) * COLS]
+            nc.sync.dma_start(
+                out=rows.rearrange("(u p) c -> p u c", p=ROWS), in_=staged[:].rearrange("p (u c) -> p u c", u=2)
+            )
+
+        for s, m0 in ((2, 0), (2, 2), (3, 0)):
             for part in range(2):
-                paired(part, m, 2, True)
+                stacked(part, m0, s)
+        for m in range(2, ROW_TILES):
+            for part in range(2):
+                single(part, m, SLICES - 1, part == 0)

@@ -22,8 +22,8 @@ ROWS = 128
 COLS = 512
 ROW_TILES = N // ROWS
 SLICES = J // COLS
-EARLY_N = 256
-LATE_N = N - EARLY_N
+EARLY_N = ROWS
+LATE_N = 2 * ROWS
 AHEAD = 3
 
 
@@ -47,19 +47,22 @@ def tile_list_cpxtab_none_kernel(
         nc.gpsimd.memset(scale_win[0][:, T // 2 : T].bitcast(I32), 0)
         nc.vector.memset(wi_spread[:].bitcast(I32), 0)
         nc.vector.memset(scale_win[1][:].bitcast(I32), 0)
+        next_planes = keep.tile([P, 2 * COLS], U8, name="next_planes", align_bytes=64)
+        nc.vector.memset(next_planes[:].bitcast(I32), 0)
 
-        def load_words(a, table_words):
-            nc.sync.dma_start(
-                out=word_win[a][:].bitcast(I32), in_=table_words[0].rearrange("p t i -> p (t i)").bitcast(I32)
-            )
+        def load_words(a, table_words, t0, t1):
+            rows = table_words[0].rearrange("p t i -> p (t i)").bitcast(I32)
+            nc.sync.dma_start(out=word_win[a][:, t0:t1].bitcast(I32), in_=rows[:, t0:t1])
 
         nc.sync.dma_start(offsets[:], offs)
-        nc.sync.dma_start(out=wi_codes[:].bitcast(I32), in_=wi_words[0].bitcast(I32))
-        nc.sync.dma_start(out=scale_win[0][0:P:8, :].bitcast(I32), in_=tab_scales[0].bitcast(I32))
-        nc.sync.dma_start(out=wi_spread[0:P:8, :].bitcast(I32), in_=wi_scales[0].bitcast(I32))
         nc.sync.dma_start(out=raw_early[:], in_=wr_rows[:, :, 0:EARLY_N])
+        nc.sync.dma_start(out=scale_win[0][0:P:8, :].bitcast(I32), in_=tab_scales[0].bitcast(I32))
+        nc.sync.dma_start(out=wi_codes[:].bitcast(I32), in_=wi_words[0].bitcast(I32))
+        nc.sync.dma_start(out=wi_spread[0:P:8, :].bitcast(I32), in_=wi_scales[0].bitcast(I32))
+        load_words(0, tab_words, 0, T // 4)
         nc.sync.dma_start(out=scale_win[1][0:P:8, :].bitcast(I32), in_=tab2_scales[0].bitcast(I32))
-        load_words(0, tab_words)
+        load_words(0, tab_words, T // 4, T)
+        load_words(1, tab2_words, 0, T // 2)
 
         def quantise(rounded, width, name):
             codes = keep.tile([P, width], U32, name=name + "_codes", align_bytes=64)
@@ -95,64 +98,74 @@ def tile_list_cpxtab_none_kernel(
                 dst.rearrange("p (n i) -> p n i", i=PACK), raw_early[:].rearrange("p i n -> p n i"), COPY, scale=sign
             )
 
-        half_j = J // 2
-        first_planes = []
-        for a in range(2):
-            spread = keep.tile([P, half_j], U8, name="spread%d" % a, align_bytes=64)
-            gather(spread[:], scale_win[a], 0, 2)
-            made = keep.tile([P, half_j + (N if a == 0 else 0)], U8, name="first_planes%d" % a, align_bytes=64)
-            nc.vector.tensor_copy(made[:, 0:half_j].bitcast(I32), spread[:].bitcast(I32))
-            if a == 0:
-                nc.vector.tensor_copy(made[:, half_j:].bitcast(I32), wi_spread[:].bitcast(I32))
-            carry_rows(nc.sync, made)
-            if a == 0:
-                load_words(1, tab2_words)
-            first_planes.append(made)
+        first_spread = keep.tile([P, 2 * COLS], U8, name="first_spread", align_bytes=64)
+        gather(first_spread[:], scale_win[0], 0, 2)
+        first_planes = keep.tile([P, 2 * COLS + N], U8, name="first_planes", align_bytes=64)
+        nc.vector.tensor_copy(first_planes[:, 2 * COLS :].bitcast(I32), wi_spread[:].bitcast(I32))
+        nc.vector.tensor_copy(first_planes[:, 0 : 2 * COLS].bitcast(I32), first_spread[:].bitcast(I32))
+        carry_rows(nc.sync, first_planes)
+        load_words(1, tab2_words, T // 2, T)
+        raw_next = keep.tile([P, PACK, ROWS], F32, name="raw_next")
+        nc.sync.dma_start(out=raw_next[:], in_=wr_rows[:, :, ROWS : 2 * ROWS])
+
+        next_spread = keep.tile([P, 2 * COLS], U8, name="next_spread", align_bytes=64)
+        gather(next_spread[:], scale_win[1], 0, 2)
+        for r in range(4):
+            nc.sync.dma_start(out=next_planes[r:P:32, :].bitcast(I32), in_=next_spread[8 * r : P : 32, :].bitcast(I32))
         raw_late = keep.tile([P, PACK, LATE_N], F32, name="raw_late")
-        nc.sync.dma_start(out=raw_late[:], in_=wr_rows[:, :, EARLY_N:N])
-        wi_plane = first_planes[0][:, half_j:]
+        nc.sync.dma_start(out=raw_late[:], in_=wr_rows[:, :, 2 * ROWS : N])
+        wi_plane = first_planes[:, 2 * COLS :]
         for win, table_scales in zip(scale_win, (tab_scales, tab2_scales)):
             for r in range(1, 4):
                 nc.sync.dma_start(out=win[r:P:32, :].bitcast(I32), in_=table_scales[0, r:16:4, :].bitcast(I32))
-        for a in range(2):
+        for a, made in enumerate((first_planes, next_planes)):
             for s in range(2):
-                planes[a, s] = first_planes[a][:, s * COLS : (s + 1) * COLS]
+                planes[a, s] = made[:, s * COLS : (s + 1) * COLS]
 
         codes, plane = quantise(both_early, 2 * EARLY_N, "early")
-        wr_minus = [(codes[:, 0:EARLY_N], plane[:, 0:EARLY_N])]
-        wr_plus = [(codes[:, EARLY_N:], plane[:, EARLY_N:])]
+        wr_minus = [(codes[:, 0:ROWS], plane[:, 0:ROWS])]
+        wr_plus = [(codes[:, ROWS:], plane[:, ROWS:])]
         for s in range(AHEAD):
             gather_words(0, s, own_words(0, s))
         for s in range(2):
             gather_words(1, s, own_words(1, s))
 
+        both_next = keep.tile([P, 2 * PACK * ROWS], BF16, name="both_next", align_bytes=64)
+        nc.scalar.activation(
+            both_next[:, PACK * ROWS :].rearrange("p (n i) -> p n i", i=PACK),
+            raw_next[:].rearrange("p i n -> p n i"),
+            COPY,
+        )
+        nc.vector.tensor_scalar(both_next[:, 0 : PACK * ROWS], both_next[:, PACK * ROWS :], -1.0, None, MULT)
+        codes, plane = quantise(both_next, 2 * ROWS, "next")
+        wr_minus.append((codes[:, 0:ROWS], plane[:, 0:ROWS]))
+        wr_plus.append((codes[:, ROWS:], plane[:, ROWS:]))
+
         plus_late = keep.tile([P, PACK * LATE_N], BF16, name="plus_late", tag="late_a", align_bytes=64)
         minus_late = keep.tile([P, PACK * LATE_N], BF16, name="minus_late", tag="late_b", align_bytes=64)
         nc.vector.tensor_copy(interleaved(plus_late), raw_late[:].rearrange("p i n -> p n i"))
-        nc.vector.tensor_scalar(minus_late[:], plus_late[:], -1.0, None, MULT)
         codes, plane = quantise(plus_late, LATE_N, "plus_late")
-        wr_plus.append((codes[:], plane[:]))
+        wr_plus.extend((codes[:, u * ROWS : (u + 1) * ROWS], plane[:, u * ROWS : (u + 1) * ROWS]) for u in range(2))
+        nc.vector.tensor_scalar(minus_late[:], plus_late[:], -1.0, None, MULT)
         codes, plane = quantise(minus_late, LATE_N, "minus_late")
-        wr_minus.append((codes[:], plane[:]))
+        wr_minus.extend((codes[:, u * ROWS : (u + 1) * ROWS], plane[:, u * ROWS : (u + 1) * ROWS]) for u in range(2))
 
         third_words = keep.tile([P, 2 * COLS], U32, name="third_words", tag="late_a", align_bytes=64)
-        late_planes = keep.tile([P, 4 * COLS], U8, name="late_planes", tag="late_b", align_bytes=64)
+        third_planes = keep.tile([P, 2 * COLS], U8, name="third_planes", tag="late_b", align_bytes=64)
+
+        def gather_planes(s, tile):
+            for a in range(2):
+                planes[a, s] = tile[:, a * COLS : (a + 1) * COLS]
+                gather(planes[a, s], scale_win[a], s)
+
         for a in range(2):
             if (a, 2) not in words:
                 gather_words(a, 2, third_words[:, a * COLS : (a + 1) * COLS])
-        gather(late_planes[:, 0 : 2 * COLS], scale_win[0], 2, 2)
-        for s in range(2, SLICES):
-            planes[0, s] = late_planes[:, (s - 2) * COLS : (s - 1) * COLS]
-            planes[1, s] = late_planes[:, s * COLS : (s + 1) * COLS]
-            gather(planes[1, s], scale_win[1], s)
-        last_words = keep.tile([P, 2 * COLS], U32, name="last_words", tag="scale_win1", align_bytes=64)
-        for a in range(2):
-            gather_words(a, 3, last_words[:, a * COLS : (a + 1) * COLS])
+        gather_planes(2, third_planes)
 
         def wr_operand(signed, m):
-            half, col = divmod(m * ROWS, EARLY_N)
-            codes, plane = signed[half]
-            return codes[:, col : col + ROWS].bitcast(FP8X4), plane[:, col : col + ROWS]
+            codes, plane = signed[m]
+            return codes.bitcast(FP8X4), plane
 
         def wi_operand(m):
             return (
@@ -166,7 +179,7 @@ def tile_list_cpxtab_none_kernel(
                 weights = (wr_operand(wr_minus, m), wi_operand(m))
             else:
                 weights = (wi_operand(m), wr_operand(wr_plus, m))
-            order = (0, 1) if s < 2 and m < 2 else (1, 0)
+            order = (0, 1) if s < 2 and (m == 0 or (part == 1 and m < 3)) else (1, 0)
             for a in order:
                 nc.tensor.matmul_mx(
                     out=acc[:],
@@ -186,7 +199,7 @@ def tile_list_cpxtab_none_kernel(
         outs = (out_0, out_1)
 
         def staging(name, width):
-            return keep.tile([P, width], F32, name=name)
+            return keep.tile([P, width], F32, name=name, tag=name, align_bytes=64)
 
         def single(part, m, s, on_vector):
             staged = staging("staged%d_%d_%d" % (s, m, part), COLS)
@@ -201,25 +214,30 @@ def tile_list_cpxtab_none_kernel(
                 out=outs[part][m * ROWS : (m + 1) * ROWS, s0 * COLS : (s0 + 2) * COLS], in_=staged[:]
             )
 
-        for s in range(2):
-            for m in range(2):
-                for part in range(2):
-                    single(part, m, s, False)
-        for m in range(2, ROW_TILES):
-            for part in range(2):
-                paired(part, m, 0, False)
         def stacked(part, m0, s):
             staged = staging("stacked%d_%d_%d" % (s, m0, part), 2 * COLS)
             for u in range(2):
-                product(part, m0 + u, s, staged[:, u * COLS : (u + 1) * COLS], s == SLICES - 1 and u == 0)
+                product(part, m0 + u, s, staged[:, u * COLS : (u + 1) * COLS], (s, m0, part) >= (2, 2, 1) and u == 0)
             rows = outs[part][m0 * ROWS : (m0 + 2) * ROWS, s * COLS : (s + 1) * COLS]
             nc.sync.dma_start(
                 out=rows.rearrange("(u p) c -> p u c", p=ROWS), in_=staged[:].rearrange("p (u c) -> p u c", u=2)
             )
 
+        for s in range(2):
+            for part in range(2):
+                single(part, 0, s, False)
+
+        last_planes = keep.tile([P, 2 * COLS], U8, name="last_planes", tag="staged0_0_0", align_bytes=64)
+        gather_planes(3, last_planes)
+        last_words = keep.tile([P, 2 * COLS], U32, name="last_words", tag="scale_win1", align_bytes=64)
+        for a in range(2):
+            gather_words(a, 3, last_words[:, a * COLS : (a + 1) * COLS])
+
+        for m, part in ((1, 1), (2, 1), (1, 0), (2, 0), (3, 1), (3, 0)):
+            paired(part, m, 0, False)
         for s, m0 in ((2, 0), (2, 2), (3, 0)):
             for part in range(2):
                 stacked(part, m0, s)
+        stacked(0, 2, 3)
         for m in range(2, ROW_TILES):
-            for part in range(2):
-                single(part, m, SLICES - 1, part == 0)
+            single(1, m, SLICES - 1, m == 2)

@@ -64,8 +64,8 @@ def tile_list_cpxtab_none_kernel(
         load_words(0, tab_words, T // 4, T)
         load_words(1, tab2_words, 0, T // 2)
 
-        def quantise(rounded, width, name):
-            codes = keep.tile([P, width], U32, name=name + "_codes", align_bytes=64)
+        def quantise(rounded, width, name, tag=None):
+            codes = keep.tile([P, width], U32, name=name + "_codes", tag=tag or name + "_codes", align_bytes=64)
             plane = keep.tile([P, width], U8, name=name + "_plane", align_bytes=64)
             nc.vector.quantize_mx(out=codes[:].bitcast(FP8X4), scales=plane[:], in_=rounded[:])
             return codes, plane
@@ -112,7 +112,7 @@ def tile_list_cpxtab_none_kernel(
         gather(next_spread[:], scale_win[1], 0, 2)
         for r in range(4):
             nc.sync.dma_start(out=next_planes[r:P:32, :].bitcast(I32), in_=next_spread[8 * r : P : 32, :].bitcast(I32))
-        raw_late = keep.tile([P, PACK, LATE_N], F32, name="raw_late")
+        raw_late = keep.tile([P, PACK, LATE_N], F32, name="raw_late", tag="raw_late", align_bytes=64)
         nc.sync.dma_start(out=raw_late[:], in_=wr_rows[:, :, 2 * ROWS : N])
         wi_plane = first_planes[:, 2 * COLS :]
         for win, table_scales in zip(scale_win, (tab_scales, tab2_scales)):
@@ -130,28 +130,24 @@ def tile_list_cpxtab_none_kernel(
         for s in range(2):
             gather_words(1, s, own_words(1, s))
 
-        both_next = keep.tile([P, 2 * PACK * ROWS], BF16, name="both_next", align_bytes=64)
-        nc.scalar.activation(
-            both_next[:, PACK * ROWS :].rearrange("p (n i) -> p n i", i=PACK),
-            raw_next[:].rearrange("p i n -> p n i"),
-            COPY,
-        )
-        nc.vector.tensor_scalar(both_next[:, 0 : PACK * ROWS], both_next[:, PACK * ROWS :], -1.0, None, MULT)
-        codes, plane = quantise(both_next, 2 * ROWS, "next")
-        wr_minus.append((codes[:, 0:ROWS], plane[:, 0:ROWS]))
-        wr_plus.append((codes[:, ROWS:], plane[:, ROWS:]))
+        plus_next = keep.tile([P, PACK * ROWS], BF16, name="plus_next", align_bytes=64)
+        nc.scalar.activation(interleaved(plus_next), raw_next[:].rearrange("p i n -> p n i"), COPY)
+        codes, plane = quantise(plus_next, ROWS, "plus_next")
+        wr_plus.append((codes[:], plane[:]))
 
         plus_late = keep.tile([P, PACK * LATE_N], BF16, name="plus_late", tag="late_a", align_bytes=64)
-        minus_late = keep.tile([P, PACK * LATE_N], BF16, name="minus_late", tag="late_b", align_bytes=64)
         nc.vector.tensor_copy(interleaved(plus_late), raw_late[:].rearrange("p i n -> p n i"))
-        codes, plane = quantise(plus_late, LATE_N, "plus_late")
-        wr_plus.extend((codes[:, u * ROWS : (u + 1) * ROWS], plane[:, u * ROWS : (u + 1) * ROWS]) for u in range(2))
-        nc.vector.tensor_scalar(minus_late[:], plus_late[:], -1.0, None, MULT)
-        codes, plane = quantise(minus_late, LATE_N, "minus_late")
-        wr_minus.extend((codes[:, u * ROWS : (u + 1) * ROWS], plane[:, u * ROWS : (u + 1) * ROWS]) for u in range(2))
+        minus_rest = keep.tile([P, PACK * (ROWS + LATE_N)], BF16, name="minus_rest", tag="raw_late", align_bytes=64)
+        nc.vector.tensor_scalar(minus_rest[:, 0 : PACK * ROWS], plus_next[:], -1.0, None, MULT)
+        nc.vector.tensor_scalar(minus_rest[:, PACK * ROWS :], plus_late[:], -1.0, None, MULT)
+        for signed, rounded, count, name in ((wr_plus, plus_late, 2, "plus_late"), (wr_minus, minus_rest, 3, "minus_rest")):
+            codes, plane = quantise(rounded, count * ROWS, name)
+            signed.extend(
+                (codes[:, u * ROWS : (u + 1) * ROWS], plane[:, u * ROWS : (u + 1) * ROWS]) for u in range(count)
+            )
 
         third_words = keep.tile([P, 2 * COLS], U32, name="third_words", tag="late_a", align_bytes=64)
-        third_planes = keep.tile([P, 2 * COLS], U8, name="third_planes", tag="late_b", align_bytes=64)
+        third_planes = keep.tile([P, 2 * COLS], U8, name="third_planes", tag="raw_late", align_bytes=64)
 
         def gather_planes(s, tile):
             for a in range(2):
@@ -173,23 +169,37 @@ def tile_list_cpxtab_none_kernel(
                 wi_plane[:, m * ROWS : (m + 1) * ROWS],
             )
 
-        def product(part, m, s, dst, on_vector):
-            acc = psum.tile([P, COLS], F32, name="acc")
+        def one_pass(acc, part, m, s, a, start):
             if part == 0:
                 weights = (wr_operand(wr_minus, m), wi_operand(m))
             else:
                 weights = (wi_operand(m), wr_operand(wr_plus, m))
-            order = (0, 1) if s < 2 and (m == 0 or (part == 1 and m < 3)) else (1, 0)
-            for a in order:
-                nc.tensor.matmul_mx(
-                    out=acc[:],
-                    lhsT=weights[a][0],
-                    lhsT_scale=weights[a][1],
-                    rhs=words[a, s].bitcast(FP8X4),
-                    rhs_scale=planes[a, s],
-                    start=(a == order[0]),
-                    stop=(a == order[1]),
-                )
+            nc.tensor.matmul_mx(
+                out=acc[:],
+                lhsT=weights[a][0],
+                lhsT_scale=weights[a][1],
+                rhs=words[a, s].bitcast(FP8X4),
+                rhs_scale=planes[a, s],
+                start=start,
+                stop=not start,
+            )
+
+        opened = {}
+
+        def open_on_tab(part, m, s):
+            opened[part, m, s] = psum.tile([P, COLS], F32, name="acc")
+            one_pass(opened[part, m, s], part, m, s, 0, True)
+
+        def product(part, m, s, dst, on_vector):
+            if s < 2 and (m == 0 or (part == 1 and m < 3)):
+                open_on_tab(part, m, s)
+            if (part, m, s) in opened:
+                acc = opened[part, m, s]
+                one_pass(acc, part, m, s, 1, False)
+            else:
+                acc = psum.tile([P, COLS], F32, name="acc")
+                one_pass(acc, part, m, s, 1, True)
+                one_pass(acc, part, m, s, 0, False)
             sign = -1.0 if part == 0 else 1.0
             if on_vector:
                 nc.vector.tensor_scalar(dst, acc[:], sign, None, MULT)
@@ -235,9 +245,14 @@ def tile_list_cpxtab_none_kernel(
 
         for m, part in ((1, 1), (2, 1), (1, 0), (2, 0), (3, 1), (3, 0)):
             paired(part, m, 0, False)
-        for s, m0 in ((2, 0), (2, 2), (3, 0)):
+        for m0 in (0, 2):
             for part in range(2):
-                stacked(part, m0, s)
+                stacked(part, m0, 2)
+        for part in range(2):
+            for m in range(2):
+                open_on_tab(part, m, 3)
+        for part in range(2):
+            stacked(part, 0, 3)
         stacked(0, 2, 3)
         for m in range(2, ROW_TILES):
             single(1, m, SLICES - 1, m == 2)

@@ -135,19 +135,21 @@ def tile_list_cpxtab_none_kernel(
         codes, plane = quantise(plus_next, ROWS, "plus_next")
         wr_plus.append((codes[:], plane[:]))
 
+        minus_next = keep.tile([P, PACK * ROWS], BF16, name="minus_next", align_bytes=64)
+        nc.vector.tensor_scalar(minus_next[:], plus_next[:], -1.0, None, MULT)
+        codes, plane = quantise(minus_next, ROWS, "minus_next")
+        wr_minus.append((codes[:], plane[:]))
+
         plus_late = keep.tile([P, PACK * LATE_N], BF16, name="plus_late", tag="late_a", align_bytes=64)
+        minus_late = keep.tile([P, PACK * LATE_N], BF16, name="minus_late", tag="late_b", align_bytes=64)
         nc.vector.tensor_copy(interleaved(plus_late), raw_late[:].rearrange("p i n -> p n i"))
-        minus_rest = keep.tile([P, PACK * (ROWS + LATE_N)], BF16, name="minus_rest", tag="raw_late", align_bytes=64)
-        nc.vector.tensor_scalar(minus_rest[:, 0 : PACK * ROWS], plus_next[:], -1.0, None, MULT)
-        nc.vector.tensor_scalar(minus_rest[:, PACK * ROWS :], plus_late[:], -1.0, None, MULT)
-        for signed, rounded, count, name in ((wr_plus, plus_late, 2, "plus_late"), (wr_minus, minus_rest, 3, "minus_rest")):
-            codes, plane = quantise(rounded, count * ROWS, name)
-            signed.extend(
-                (codes[:, u * ROWS : (u + 1) * ROWS], plane[:, u * ROWS : (u + 1) * ROWS]) for u in range(count)
-            )
+        nc.vector.tensor_scalar(minus_late[:], plus_late[:], -1.0, None, MULT)
+        for signed, rounded, name in ((wr_plus, plus_late, "plus_late"), (wr_minus, minus_late, "minus_late")):
+            codes, plane = quantise(rounded, LATE_N, name)
+            signed.extend((codes[:, u * ROWS : (u + 1) * ROWS], plane[:, u * ROWS : (u + 1) * ROWS]) for u in range(2))
 
         third_words = keep.tile([P, 2 * COLS], U32, name="third_words", tag="late_a", align_bytes=64)
-        third_planes = keep.tile([P, 2 * COLS], U8, name="third_planes", tag="raw_late", align_bytes=64)
+        third_planes = keep.tile([P, 2 * COLS], U8, name="third_planes", tag="late_b", align_bytes=64)
 
         def gather_planes(s, tile):
             for a in range(2):
@@ -243,7 +245,7 @@ def tile_list_cpxtab_none_kernel(
         for a in range(2):
             gather_words(a, 3, last_words[:, a * COLS : (a + 1) * COLS])
 
-        for m, part in ((1, 1), (2, 1), (1, 0), (2, 0), (3, 1), (3, 0)):
+        for m, part in ((1, 1), (1, 0), (2, 1), (3, 1), (2, 0), (3, 0)):
             paired(part, m, 0, False)
         for m0 in (0, 2):
             for part in range(2):

@@ -59,9 +59,8 @@ def tile_list_cpxtab_none_kernel(
         nc.sync.dma_start(out=scale_win[0][0:P:8, :].bitcast(I32), in_=tab_scales[0].bitcast(I32))
         nc.sync.dma_start(out=wi_codes[:].bitcast(I32), in_=wi_words[0].bitcast(I32))
         nc.sync.dma_start(out=wi_spread[0:P:8, :].bitcast(I32), in_=wi_scales[0].bitcast(I32))
-        load_words(0, tab_words, 0, T // 4)
-        nc.sync.dma_start(out=scale_win[1][0:P:8, :].bitcast(I32), in_=tab2_scales[0].bitcast(I32))
-        load_words(0, tab_words, T // 4, T)
+        nc.sync.dma_start(out=scale_win[1][4:P:8, :].bitcast(I32), in_=tab2_scales[0].bitcast(I32))
+        load_words(0, tab_words, 0, T)
         load_words(1, tab2_words, 0, T // 2)
 
         def quantise(rounded, width, name, tag=None):
@@ -111,12 +110,12 @@ def tile_list_cpxtab_none_kernel(
         next_spread = keep.tile([P, 2 * COLS], U8, name="next_spread", align_bytes=64)
         gather(next_spread[:], scale_win[1], 0, 2)
         for r in range(4):
-            nc.sync.dma_start(out=next_planes[r:P:32, :].bitcast(I32), in_=next_spread[8 * r : P : 32, :].bitcast(I32))
+            nc.sync.dma_start(out=next_planes[r:P:32, :].bitcast(I32), in_=next_spread[8 * r + 4 : P : 32, :].bitcast(I32))
         raw_late = keep.tile([P, PACK, LATE_N], F32, name="raw_late", tag="raw_late", align_bytes=64)
         nc.sync.dma_start(out=raw_late[:], in_=wr_rows[:, :, 2 * ROWS : N])
         wi_plane = first_planes[:, 2 * COLS :]
-        for win, table_scales in zip(scale_win, (tab_scales, tab2_scales)):
-            for r in range(1, 4):
+        for win, table_scales, placed in zip(scale_win, (tab_scales, tab2_scales), (1, 0)):
+            for r in range(placed, 4):
                 nc.sync.dma_start(out=win[r:P:32, :].bitcast(I32), in_=table_scales[0, r:16:4, :].bitcast(I32))
         for a, made in enumerate((first_planes, next_planes)):
             for s in range(2):

@@ -69,8 +69,11 @@ def tile_list_cpxtab_none_kernel(
             nc.vector.quantize_mx(out=codes[:].bitcast(FP8X4), scales=plane[:], in_=rounded[:])
             return codes, plane
 
-        def interleaved(rounded):
-            return rounded[:].rearrange("p (n i) -> p n i", i=PACK)
+        def by_fours(rounded):
+            return rounded.rearrange("p (c n i) -> p c i n", n=4, i=PACK)
+
+        def rows_by_fours(raw):
+            return raw[:].rearrange("p i (c n) -> p c i n", n=4)
 
         def gather(dst, win, s, count=1):
             nc.vector.tensor_copy(dst, win[:].indirect(offsets[:, s * (COLS // 16) : (s + count) * (COLS // 16)]))
@@ -129,19 +132,17 @@ def tile_list_cpxtab_none_kernel(
         for s in range(2):
             gather_words(1, s, own_words(1, s))
 
-        plus_next = keep.tile([P, PACK * ROWS], BF16, name="plus_next", align_bytes=64)
-        nc.scalar.activation(interleaved(plus_next), raw_next[:].rearrange("p i n -> p n i"), COPY)
-        codes, plane = quantise(plus_next, ROWS, "plus_next")
-        wr_plus.append((codes[:], plane[:]))
-
-        minus_next = keep.tile([P, PACK * ROWS], BF16, name="minus_next", align_bytes=64)
-        nc.vector.tensor_scalar(minus_next[:], plus_next[:], -1.0, None, MULT)
-        codes, plane = quantise(minus_next, ROWS, "minus_next")
-        wr_minus.append((codes[:], plane[:]))
+        both_next = keep.tile([P, 2 * PACK * ROWS], BF16, name="both_next", align_bytes=64)
+        for half, sign in enumerate((1.0, -1.0)):
+            dst = both_next[:, half * PACK * ROWS : (half + 1) * PACK * ROWS]
+            nc.scalar.activation(by_fours(dst), rows_by_fours(raw_next), COPY, scale=sign)
+        codes, plane = quantise(both_next, 2 * ROWS, "next")
+        wr_plus.append((codes[:, 0:ROWS], plane[:, 0:ROWS]))
+        wr_minus.append((codes[:, ROWS:], plane[:, ROWS:]))
 
         plus_late = keep.tile([P, PACK * LATE_N], BF16, name="plus_late", tag="late_a", align_bytes=64)
         minus_late = keep.tile([P, PACK * LATE_N], BF16, name="minus_late", tag="late_b", align_bytes=64)
-        nc.vector.tensor_copy(interleaved(plus_late), raw_late[:].rearrange("p i n -> p n i"))
+        nc.vector.tensor_copy(by_fours(plus_late[:]), rows_by_fours(raw_late))
         nc.vector.tensor_scalar(minus_late[:], plus_late[:], -1.0, None, MULT)
         for signed, rounded, name in ((wr_plus, plus_late, "plus_late"), (wr_minus, minus_late, "minus_late")):
             codes, plane = quantise(rounded, LATE_N, name)

@@ -140,27 +140,6 @@ def tile_list_cpxtab_none_kernel(
         wr_plus.append((codes[:, 0:ROWS], plane[:, 0:ROWS]))
         wr_minus.append((codes[:, ROWS:], plane[:, ROWS:]))
 
-        plus_late = keep.tile([P, PACK * LATE_N], BF16, name="plus_late", tag="late_a", align_bytes=64)
-        minus_late = keep.tile([P, PACK * LATE_N], BF16, name="minus_late", tag="late_b", align_bytes=64)
-        nc.vector.tensor_copy(by_fours(plus_late[:]), rows_by_fours(raw_late))
-        nc.vector.tensor_scalar(minus_late[:], plus_late[:], -1.0, None, MULT)
-        for signed, rounded, name in ((wr_plus, plus_late, "plus_late"), (wr_minus, minus_late, "minus_late")):
-            codes, plane = quantise(rounded, LATE_N, name)
-            signed.extend((codes[:, u * ROWS : (u + 1) * ROWS], plane[:, u * ROWS : (u + 1) * ROWS]) for u in range(2))
-
-        third_words = keep.tile([P, 2 * COLS], U32, name="third_words", tag="late_a", align_bytes=64)
-        third_planes = keep.tile([P, 2 * COLS], U8, name="third_planes", tag="late_b", align_bytes=64)
-
-        def gather_planes(s, tile):
-            for a in range(2):
-                planes[a, s] = tile[:, a * COLS : (a + 1) * COLS]
-                gather(planes[a, s], scale_win[a], s)
-
-        for a in range(2):
-            if (a, 2) not in words:
-                gather_words(a, 2, third_words[:, a * COLS : (a + 1) * COLS])
-        gather_planes(2, third_planes)
-
         def wr_operand(signed, m):
             codes, plane = signed[m]
             return codes.bitcast(FP8X4), plane
@@ -219,9 +198,11 @@ def tile_list_cpxtab_none_kernel(
             nc.sync.dma_start(out=outs[part][m * ROWS : (m + 1) * ROWS, s * COLS : (s + 1) * COLS], in_=staged[:])
 
         def paired(part, m, s0, vector_too):
-            staged = staging("paired%d_%d_%d" % (s0, m, part), 2 * COLS)
+            name = "paired%d_%d_%d" % (s0, m, part)
+            tag = "raw_late" if vector_too else name
+            staged = keep.tile([P, 2 * COLS], F32, name=name, tag=tag, align_bytes=64)
             for u in range(2):
-                product(part, m, s0 + u, staged[:, u * COLS : (u + 1) * COLS], vector_too and u == 1)
+                product(part, m, s0 + u, staged[:, u * COLS : (u + 1) * COLS], vector_too and u == 0)
             nc.sync.dma_start(
                 out=outs[part][m * ROWS : (m + 1) * ROWS, s0 * COLS : (s0 + 2) * COLS], in_=staged[:]
             )
@@ -239,13 +220,35 @@ def tile_list_cpxtab_none_kernel(
             for part in range(2):
                 single(part, 0, s, False)
 
+        plus_late = keep.tile([P, PACK * LATE_N], BF16, name="plus_late", tag="late_a", align_bytes=64)
+        minus_late = keep.tile([P, PACK * LATE_N], BF16, name="minus_late", tag="late_b", align_bytes=64)
+        nc.vector.tensor_copy(by_fours(plus_late[:]), rows_by_fours(raw_late))
+        nc.vector.tensor_scalar(minus_late[:], plus_late[:], -1.0, None, MULT)
+        paired(1, 1, 0, True)
+        for signed, rounded, name in ((wr_plus, plus_late, "plus_late"), (wr_minus, minus_late, "minus_late")):
+            codes, plane = quantise(rounded, LATE_N, name)
+            signed.extend((codes[:, u * ROWS : (u + 1) * ROWS], plane[:, u * ROWS : (u + 1) * ROWS]) for u in range(2))
+
+        third_words = keep.tile([P, 2 * COLS], U32, name="third_words", tag="late_a", align_bytes=64)
+        third_planes = keep.tile([P, 2 * COLS], U8, name="third_planes", tag="late_b", align_bytes=64)
+
+        def gather_planes(s, tile):
+            for a in range(2):
+                planes[a, s] = tile[:, a * COLS : (a + 1) * COLS]
+                gather(planes[a, s], scale_win[a], s)
+
+        for a in range(2):
+            if (a, 2) not in words:
+                gather_words(a, 2, third_words[:, a * COLS : (a + 1) * COLS])
+        gather_planes(2, third_planes)
+
         last_planes = keep.tile([P, 2 * COLS], U8, name="last_planes", tag="staged0_0_0", align_bytes=64)
         gather_planes(3, last_planes)
         last_words = keep.tile([P, 2 * COLS], U32, name="last_words", tag="scale_win1", align_bytes=64)
         for a in range(2):
             gather_words(a, 3, last_words[:, a * COLS : (a + 1) * COLS])
 
-        for m, part in ((1, 1), (1, 0), (2, 1), (3, 1), (2, 0), (3, 0)):
+        for m, part in ((1, 0), (2, 1), (3, 1), (2, 0), (3, 0)):
             paired(part, m, 0, False)
         for m0 in (0, 2):
             for part in range(2):

@@ -61,7 +61,7 @@ def tile_list_cpxtab_none_kernel(
         nc.sync.dma_start(out=wi_spread[0:P:8, :].bitcast(I32), in_=wi_scales[0].bitcast(I32))
         nc.sync.dma_start(out=scale_win[1][4:P:8, :].bitcast(I32), in_=tab2_scales[0].bitcast(I32))
         load_words(0, tab_words, 0, T)
-        load_words(1, tab2_words, 0, T // 2)
+        load_words(1, tab2_words, 0, 3 * T // 8)
 
         def quantise(rounded, width, name, tag=None):
             codes = keep.tile([P, width], U32, name=name + "_codes", tag=tag or name + "_codes", align_bytes=64)
@@ -106,7 +106,7 @@ def tile_list_cpxtab_none_kernel(
         nc.vector.tensor_copy(first_planes[:, 2 * COLS :].bitcast(I32), wi_spread[:].bitcast(I32))
         nc.vector.tensor_copy(first_planes[:, 0 : 2 * COLS].bitcast(I32), first_spread[:].bitcast(I32))
         carry_rows(nc.sync, first_planes)
-        load_words(1, tab2_words, T // 2, T)
+        load_words(1, tab2_words, 3 * T // 8, T)
         raw_next = keep.tile([P, PACK, ROWS], F32, name="raw_next")
         nc.sync.dma_start(out=raw_next[:], in_=wr_rows[:, :, ROWS : 2 * ROWS])
 

@@ -39,13 +39,12 @@ def tile_list_cpxtab_none_kernel(
         word_win = [keep.tile([P, T], U32, name="word_win%d" % a, align_bytes=64) for a in range(2)]
         scale_win = [keep.tile([P, T], U8, name="scale_win%d" % a, tag="scale_win%d" % a, align_bytes=64) for a in range(2)]
         wi_codes = keep.tile([P, 2 * N], U8, name="wi_codes", align_bytes=64)
-        wi_spread = keep.tile([P, N], U8, name="wi_spread", align_bytes=64)
+        first_planes = keep.tile([P, 2 * COLS + N], U8, name="first_planes", align_bytes=64)
         wr_rows = wr.rearrange("(p i) n -> p i n", i=PACK)
         raw_early = keep.tile([P, PACK, EARLY_N], F32, name="raw_early", tag="early", align_bytes=64)
 
-        nc.vector.memset(scale_win[0][:, 0 : T // 2].bitcast(I32), 0)
-        nc.gpsimd.memset(scale_win[0][:, T // 2 : T].bitcast(I32), 0)
-        nc.vector.memset(wi_spread[:].bitcast(I32), 0)
+        nc.vector.memset(first_planes[:, 2 * COLS :].bitcast(I32), 0)
+        nc.vector.memset(scale_win[0][:].bitcast(I32), 0)
         nc.vector.memset(scale_win[1][:].bitcast(I32), 0)
         next_planes = keep.tile([P, 2 * COLS], U8, name="next_planes", align_bytes=64)
         nc.vector.memset(next_planes[:].bitcast(I32), 0)
@@ -56,10 +55,10 @@ def tile_list_cpxtab_none_kernel(
 
         nc.sync.dma_start(offsets[:], offs)
         nc.sync.dma_start(out=raw_early[:], in_=wr_rows[:, :, 0:EARLY_N])
+        nc.sync.dma_start(out=first_planes[0:P:8, 2 * COLS :].bitcast(I32), in_=wi_scales[0].bitcast(I32))
         nc.sync.dma_start(out=scale_win[0][0:P:8, :].bitcast(I32), in_=tab_scales[0].bitcast(I32))
         nc.sync.dma_start(out=wi_codes[:].bitcast(I32), in_=wi_words[0].bitcast(I32))
-        nc.sync.dma_start(out=wi_spread[0:P:8, :].bitcast(I32), in_=wi_scales[0].bitcast(I32))
-        nc.sync.dma_start(out=scale_win[1][4:P:8, :].bitcast(I32), in_=tab2_scales[0].bitcast(I32))
+        nc.sync.dma_start(out=scale_win[1][11 : 11 + 7 * 16 : 7, :].bitcast(I32), in_=tab2_scales[0].bitcast(I32))
         load_words(0, tab_words, 0, T)
         load_words(1, tab2_words, 0, 3 * T // 8)
 
@@ -102,8 +101,6 @@ def tile_list_cpxtab_none_kernel(
 
         first_spread = keep.tile([P, 2 * COLS], U8, name="first_spread", align_bytes=64)
         gather(first_spread[:], scale_win[0], 0, 2)
-        first_planes = keep.tile([P, 2 * COLS + N], U8, name="first_planes", align_bytes=64)
-        nc.vector.tensor_copy(first_planes[:, 2 * COLS :].bitcast(I32), wi_spread[:].bitcast(I32))
         nc.vector.tensor_copy(first_planes[:, 0 : 2 * COLS].bitcast(I32), first_spread[:].bitcast(I32))
         carry_rows(nc.sync, first_planes)
         load_words(1, tab2_words, 3 * T // 8, T)
@@ -113,7 +110,7 @@ def tile_list_cpxtab_none_kernel(
         next_spread = keep.tile([P, 2 * COLS], U8, name="next_spread", align_bytes=64)
         gather(next_spread[:], scale_win[1], 0, 2)
         for r in range(4):
-            nc.sync.dma_start(out=next_planes[r:P:32, :].bitcast(I32), in_=next_spread[8 * r + 4 : P : 32, :].bitcast(I32))
+            nc.sync.dma_start(out=next_planes[r:P:32, :].bitcast(I32), in_=next_spread[11 + 7 * r : 11 + 7 * 16 : 28, :].bitcast(I32))
         raw_late = keep.tile([P, PACK, LATE_N], F32, name="raw_late", tag="raw_late", align_bytes=64)
         nc.sync.dma_start(out=raw_late[:], in_=wr_rows[:, :, 2 * ROWS : N])
         wi_plane = first_planes[:, 2 * COLS :]

from contextlib import ExitStack

import concourse.mybir as mybir

K, N, T, J = 512, 512, 4096, 2048
FLOPS = 4 * 2 * K * N * J

F32 = mybir.dt.float32
BF16 = mybir.dt.bfloat16
I32 = mybir.dt.int32
U32 = mybir.dt.uint32
U16 = mybir.dt.uint16
U8 = mybir.dt.uint8
FP8X4 = mybir.dt.float8_e4m3fn_x4
FP4X4 = mybir.dt.float4_e2m1fn_x4
COPY = mybir.ActivationFunctionType.Copy
MULT = mybir.AluOpType.mult

P = 128
PACK = 4
ROWS = 128
COLS = 512
ROW_TILES = N // ROWS
SLICES = J // COLS
EARLY_N = ROWS
LATE_N = 2 * ROWS
AHEAD = 3


def tile_list_cpxtab_none_kernel(
    tc, tab_words, tab_scales, tab2_words, tab2_scales, wr, wi_words, wi_scales, offs, out_0, out_1
):
    nc = tc.nc
    with ExitStack() as ctx:
        keep = ctx.enter_context(tc.tile_pool(name="keep", bufs=1))
        psum = ctx.enter_context(tc.psum_pool(name="psum", bufs=8))

        offsets = keep.tile([P, J // 16], U16, name="offsets")
        word_win = [keep.tile([P, T], U32, name="word_win%d" % a, align_bytes=64) for a in range(2)]
        scale_win = [keep.tile([P, T], U8, name="scale_win%d" % a, tag="scale_win%d" % a, align_bytes=64) for a in range(2)]
        wi_codes = keep.tile([P, 2 * N], U8, name="wi_codes", align_bytes=64)
        first_planes = keep.tile([P, 2 * COLS + N], U8, name="first_planes", align_bytes=64)
        wr_rows = wr.rearrange("(p i) n -> p i n", i=PACK)
        raw_early = keep.tile([P, PACK, EARLY_N], F32, name="raw_early", tag="early", align_bytes=64)

        nc.vector.memset(first_planes[:, 2 * COLS :].bitcast(I32), 0)
        nc.vector.memset(scale_win[0][:].bitcast(I32), 0)
        nc.vector.memset(scale_win[1][:].bitcast(I32), 0)
        next_planes = keep.tile([P, 2 * COLS], U8, name="next_planes", align_bytes=64)
        nc.vector.memset(next_planes[:].bitcast(I32), 0)

        def load_words(a, table_words, t0, t1):
            rows = table_words[0].rearrange("p t i -> p (t i)").bitcast(I32)
            nc.sync.dma_start(out=word_win[a][:, t0:t1].bitcast(I32), in_=rows[:, t0:t1])

        nc.sync.dma_start(offsets[:], offs)
        nc.sync.dma_start(out=raw_early[:], in_=wr_rows[:, :, 0:EARLY_N])
        nc.sync.dma_start(out=first_planes[0:P:8, 2 * COLS :].bitcast(I32), in_=wi_scales[0].bitcast(I32))
        nc.sync.dma_start(out=scale_win[0][0:P:8, :].bitcast(I32), in_=tab_scales[0].bitcast(I32))
        nc.sync.dma_start(out=wi_codes[:].bitcast(I32), in_=wi_words[0].bitcast(I32))
        nc.sync.dma_start(out=scale_win[1][11 : 11 + 7 * 16 : 7, :].bitcast(I32), in_=tab2_scales[0].bitcast(I32))
        load_words(0, tab_words, 0, T)
        load_words(1, tab2_words, 0, 3 * T // 8)

        def quantise(rounded, width, name, tag=None):
            codes = keep.tile([P, width], U32, name=name + "_codes", tag=tag or name + "_codes", align_bytes=64)
            plane = keep.tile([P, width], U8, name=name + "_plane", align_bytes=64)
            nc.vector.quantize_mx(out=codes[:].bitcast(FP8X4), scales=plane[:], in_=rounded[:])
            return codes, plane

        def by_fours(rounded):
            return rounded.rearrange("p (c n i) -> p c i n", n=4, i=PACK)

        def rows_by_fours(raw):
            return raw[:].rearrange("p i (c n) -> p c i n", n=4)

        def gather(dst, win, s, count=1):
            nc.vector.tensor_copy(dst, win[:].indirect(offsets[:, s * (COLS // 16) : (s + count) * (COLS // 16)]))

        def carry_rows(queue, tile):
            for r in range(1, 4):
                queue.dma_start(out=tile[r:P:32, :].bitcast(I32), in_=tile[8 * r : P : 32, :].bitcast(I32))

        words = {}
        planes = {}

        def gather_words(a, s, dst):
            words[a, s] = dst
            gather(dst, word_win[a], s)

        def own_words(a, s):
            t = keep.tile([P, COLS], U32, name="words%d_%d" % (a, s), align_bytes=64)
            return t[:]

        both_early = keep.tile([P, 2 * PACK * EARLY_N], BF16, name="both_early", align_bytes=64)
        for half, sign in enumerate((-1.0, 1.0)):
            dst = both_early[:, half * PACK * EARLY_N : (half + 1) * PACK * EARLY_N]
            nc.scalar.activation(
                dst.rearrange("p (n i) -> p n i", i=PACK), raw_early[:].rearrange("p i n -> p n i"), COPY, scale=sign
            )

        first_spread = keep.tile([P, 2 * COLS], U8, name="first_spread", align_bytes=64)
        gather(first_spread[:], scale_win[0], 0, 2)
        nc.vector.tensor_copy(first_planes[:, 0 : 2 * COLS].bitcast(I32), first_spread[:].bitcast(I32))
        carry_rows(nc.sync, first_planes)
        load_words(1, tab2_words, 3 * T // 8, T)
        raw_next = keep.tile([P, PACK, ROWS], F32, name="raw_next")
        nc.sync.dma_start(out=raw_next[:], in_=wr_rows[:, :, ROWS : 2 * ROWS])

        next_spread = keep.tile([P, 2 * COLS], U8, name="next_spread", align_bytes=64)
        gather(next_spread[:], scale_win[1], 0, 2)
        for r in range(4):
            nc.sync.dma_start(out=next_planes[r:P:32, :].bitcast(I32), in_=next_spread[11 + 7 * r : 11 + 7 * 16 : 28, :].bitcast(I32))
        raw_late = keep.tile([P, PACK, LATE_N], F32, name="raw_late", tag="raw_late", align_bytes=64)
        nc.sync.dma_start(out=raw_late[:], in_=wr_rows[:, :, 2 * ROWS : N])
        wi_plane = first_planes[:, 2 * COLS :]
        for win, table_scales, placed in zip(scale_win, (tab_scales, tab2_scales), (1, 0)):
            for r in range(placed, 4):
                nc.sync.dma_start(out=win[r:P:32, :].bitcast(I32), in_=table_scales[0, r:16:4, :].bitcast(I32))
        for a, made in enumerate((first_planes, next_planes)):
            for s in range(2):
                planes[a, s] = made[:, s * COLS : (s + 1) * COLS]

        codes, plane = quantise(both_early, 2 * EARLY_N, "early")
        wr_minus = [(codes[:, 0:ROWS], plane[:, 0:ROWS])]
        wr_plus = [(codes[:, ROWS:], plane[:, ROWS:])]
        for s in range(AHEAD):
            gather_words(0, s, own_words(0, s))
        for s in range(2):
            gather_words(1, s, own_words(1, s))

        both_next = keep.tile([P, 2 * PACK * ROWS], BF16, name="both_next", align_bytes=64)
        for half, sign in enumerate((1.0, -1.0)):
            dst = both_next[:, half * PACK * ROWS : (half + 1) * PACK * ROWS]
            nc.scalar.activation(by_fours(dst), rows_by_fours(raw_next), COPY, scale=sign)
        codes, plane = quantise(both_next, 2 * ROWS, "next")
        wr_plus.append((codes[:, 0:ROWS], plane[:, 0:ROWS]))
        wr_minus.append((codes[:, ROWS:], plane[:, ROWS:]))

        def wr_operand(signed, m):
            codes, plane = signed[m]
            return codes.bitcast(FP8X4), plane

        def wi_operand(m):
            return (
                wi_codes[:, 2 * m * ROWS : 2 * (m + 1) * ROWS].bitcast(FP4X4),
                wi_plane[:, m * ROWS : (m + 1) * ROWS],
            )

        def one_pass(acc, part, m, s, a, start):
            if part == 0:
                weights = (wr_operand(wr_minus, m), wi_operand(m))
            else:
                weights = (wi_operand(m), wr_operand(wr_plus, m))
            nc.tensor.matmul_mx(
                out=acc[:],
                lhsT=weights[a][0],
                lhsT_scale=weights[a][1],
                rhs=words[a, s].bitcast(FP8X4),
                rhs_scale=planes[a, s],
                start=start,
                stop=not start,
            )

        opened = {}

        def open_on_tab(part, m, s):
            opened[part, m, s] = psum.tile([P, COLS], F32, name="acc")
            one_pass(opened[part, m, s], part, m, s, 0, True)

        def product(part, m, s, dst, on_vector):
            if s < 2 and (m == 0 or (part == 1 and m < 3)):
                open_on_tab(part, m, s)
            if (part, m, s) in opened:
                acc = opened[part, m, s]
                one_pass(acc, part, m, s, 1, False)
            else:
                acc = psum.tile([P, COLS], F32, name="acc")
                one_pass(acc, part, m, s, 1, True)
                one_pass(acc, part, m, s, 0, False)
            sign = -1.0 if part == 0 else 1.0
            if on_vector:
                nc.vector.tensor_scalar(dst, acc[:], sign, None, MULT)
            else:
                nc.scalar.activation(dst, acc[:], COPY, scale=sign)

        outs = (out_0, out_1)

        def staging(name, width):
            return keep.tile([P, width], F32, name=name, tag=name, align_bytes=64)

        def single(part, m, s, on_vector):
            staged = staging("staged%d_%d_%d" % (s, m, part), COLS)
            product(part, m, s, staged[:], on_vector)
            nc.sync.dma_start(out=outs[part][m * ROWS : (m + 1) * ROWS, s * COLS : (s + 1) * COLS], in_=staged[:])

        def paired(part, m, s0, vector_too):
            name = "paired%d_%d_%d" % (s0, m, part)
            tag = "raw_late" if vector_too else name
            staged = keep.tile([P, 2 * COLS], F32, name=name, tag=tag, align_bytes=64)
            for u in range(2):
                product(part, m, s0 + u, staged[:, u * COLS : (u + 1) * COLS], vector_too and u == 0)
            nc.sync.dma_start(
                out=outs[part][m * ROWS : (m + 1) * ROWS, s0 * COLS : (s0 + 2) * COLS], in_=staged[:]
            )

        def stacked(part, m0, s):
            staged = staging("stacked%d_%d_%d" % (s, m0, part), 2 * COLS)
            for u in range(2):
                product(part, m0 + u, s, staged[:, u * COLS : (u + 1) * COLS], (s, m0, part) >= (2, 2, 1) and u == 0)
            rows = outs[part][m0 * ROWS : (m0 + 2) * ROWS, s * COLS : (s + 1) * COLS]
            nc.sync.dma_start(
                out=rows.rearrange("(u p) c -> p u c", p=ROWS), in_=staged[:].rearrange("p (u c) -> p u c", u=2)
            )

        for s in range(2):
            for part in range(2):
                single(part, 0, s, False)

        plus_late = keep.tile([P, PACK * LATE_N], BF16, name="plus_late", tag="late_a", align_bytes=64)
        minus_late = keep.tile([P, PACK * LATE_N], BF16, name="minus_late", tag="late_b", align_bytes=64)
        nc.vector.tensor_copy(by_fours(plus_late[:]), rows_by_fours(raw_late))
        nc.vector.tensor_scalar(minus_late[:], plus_late[:], -1.0, None, MULT)
        paired(1, 1, 0, True)
        for signed, rounded, name in ((wr_plus, plus_late, "plus_late"), (wr_minus, minus_late, "minus_late")):
            codes, plane = quantise(rounded, LATE_N, name)
            signed.extend((codes[:, u * ROWS : (u + 1) * ROWS], plane[:, u * ROWS : (u + 1) * ROWS]) for u in range(2))

        third_words = keep.tile([P, 2 * COLS], U32, name="third_words", tag="late_a", align_bytes=64)
        third_planes = keep.tile([P, 2 * COLS], U8, name="third_planes", tag="late_b", align_bytes=64)

        def gather_planes(s, tile):
            for a in range(2):
                planes[a, s] = tile[:, a * COLS : (a + 1) * COLS]
                gather(planes[a, s], scale_win[a], s)

        for a in range(2):
            if (a, 2) not in words:
                gather_words(a, 2, third_words[:, a * COLS : (a + 1) * COLS])
        gather_planes(2, third_planes)

        last_planes = keep.tile([P, 2 * COLS], U8, name="last_planes", tag="staged0_0_0", align_bytes=64)
        gather_planes(3, last_planes)
        last_words = keep.tile([P, 2 * COLS], U32, name="last_words", tag="scale_win1", align_bytes=64)
        for a in range(2):
            gather_words(a, 3, last_words[:, a * COLS : (a + 1) * COLS])

        for m, part in ((1, 0), (2, 1), (3, 1), (2, 0), (3, 0)):
            paired(part, m, 0, False)
        for m0 in (0, 2):
            for part in range(2):
                stacked(part, m0, 2)
        for part in range(2):
            for m in range(2):
                open_on_tab(part, m, 3)
        for part in range(2):
            stacked(part, 0, 3)
        stacked(0, 2, 3)
        for m in range(2, ROW_TILES):
            single(1, m, SLICES - 1, m == 2)
